import numpy as np
import ml_dtypes


def mxq(x, axis, fmt="e4m3"):
    dtype, down = {"e4m3": (ml_dtypes.float8_e4m3fn, 7), "e5m2": (ml_dtypes.float8_e5m2, 14)}[fmt]
    v = np.moveaxis(np.asarray(x, np.float32).astype(ml_dtypes.bfloat16).astype(np.float64), axis, -1)
    blocks = v.reshape(v.shape[:-1] + (-1, 32))
    amax = np.abs(blocks).max(-1, keepdims=True)
    byte = np.maximum(np.where(amax > 0, np.frexp(amax)[1] - 1 + 127, 0) - down, 1)
    scale = np.exp2(byte - 127.0)
    codes = (blocks / scale).astype(np.float32).astype(dtype).astype(np.float64)
    return np.moveaxis((codes * scale).reshape(v.shape), -1, axis)


WIDE = False


def mx_kscale(k):
    if not WIDE:
        return np.ones(k)
    levels = np.array([10, -10, 5, -5, 0])
    if k % 512:
        return np.exp2(np.random.permutation(np.resize(levels, k // 32))).repeat(32)
    a = np.empty((k // 512, 16))
    for p in range(k // 512):
        a[p, :8] = np.random.permutation(np.resize(levels, 8))
        for g in range(8):
            far = levels[np.abs(levels - a[p, g]) >= 10]
            a[p, g + 8] = far[np.random.randint(len(far))]
    return np.exp2(a.ravel()).repeat(32)


def f64(x):
    return np.asarray(x).astype(np.float64)


def striped(idx):
    return np.tile(idx.reshape(-1, 16).T, (8, 1)).astype(np.uint16)


def unstriped(offs):
    return offs[:16].T.reshape(-1).astype(np.int64)


def relu(v):
    return np.maximum(v, 0.0)


K, T, D, S, V, N = 1024, 1024, 8, 4096, 512, 128


def setup_inputs():
    n = np.random.standard_normal
    s = mx_kscale(K)[:, None]
    return {
        "xT": (n((K, T)) * s).astype(np.float32),
        "w": (n((K, N)) / np.sqrt(K) / s).astype(np.float32),
        "b": (0.3 * n((N, 1))).astype(np.float32),
        "offs": striped(np.concatenate([np.random.permutation(T)[:V] for _ in range(D)])),
    }


def reference(xT, w, b, offs):
    idx = unstriped(offs)
    x = np.empty((K, V))
    for l in range(D):
        r = l // 4 * (4 * K // D) + l % 4 + 4 * np.arange(K // D)
        x[r] = f64(xT)[r][:, idx[l * V:(l + 1) * V]]
    xq = mxq(x, 0, "e4m3")
    return relu((mxq(f64(w), 0, "e4m3").T @ xq) + f64(b))

@@ -1,0 +1,145 @@
+from contextlib import ExitStack
+
+import concourse.mybir as mybir
+
+K, T, D, V, N = 1024, 1024, 8, 512, 128
+FLOPS = 2 * K * N * V
+F32 = mybir.dt.float32
+BF16 = mybir.dt.bfloat16
+U32 = mybir.dt.uint32
+U16 = mybir.dt.uint16
+U8 = mybir.dt.uint8
+FP8X4 = mybir.dt.float8_e4m3fn_x4
+COPY = mybir.ActivationFunctionType.Copy
+RELU = mybir.ActivationFunctionType.Relu
+MULT, ADD, MAX = mybir.AluOpType.mult, mybir.AluOpType.add, mybir.AluOpType.max
+P = 128
+
+
+def tile_picked_grid_lin_relu_sub_l_kernel(tc, xT, w, b, offs, out):
+    nc = tc.nc
+    with ExitStack() as ctx:
+        keep = ctx.enter_context(tc.tile_pool(name="keep", bufs=1))
+        psum = ctx.enter_context(tc.psum_pool(name="psum", bufs=1))
+        offsets = keep.tile([P, D * V // 16], U16, name="offsets")
+        nc.sync.dma_start(offsets[:], offs)
+        bias = keep.tile([P, 1], F32, name="bias")
+        warm = keep.tile([P, 1], F32, name="warm")
+        warm2 = keep.tile([P, 1], F32, name="warm2")
+        xrows = xT.rearrange("(g p j) c -> g j p c", g=2, j=4)
+        wrows = w.rearrange("(g p j) m -> g p j m", g=2, j=4)
+        tables = {}
+        for l in range(D):
+            tables[l] = keep.tile([P, T], F32, name="table%d" % l)
+        wraw = keep.tile([P, 2, 4, N], F32, name="wraw")
+        wg = keep.tile([P, 2, N, 4], BF16, name="wg", align_bytes=64)
+        wcodes = keep.tile([P, 2, N], U32, name="wcodes", align_bytes=64)
+        wscales = keep.tile([P, 2, N], U8, name="wscales", align_bytes=64)
+        g4 = {}
+        grouped = {}
+        codes = {}
+        scales = {}
+        for g in (0, 1):
+            g4[g] = keep.tile([P, 4, V], F32, name="g4_%d" % g)
+            grouped[g] = keep.tile([P, V, 4], BF16, name="grouped%d" % g, align_bytes=64)
+            codes[g] = keep.tile([P, V], U32, name="codes%d" % g, align_bytes=64)
+            scales[g] = keep.tile([P, V], U8, name="scales%d" % g, align_bytes=64)
+        banks = [psum.tile([P, 512], F32, name="bank%d" % c) for c in range(4)]
+        res = keep.tile([P, V], F32, name="res")
+        win = {}
+
+        def load(l):
+            nc.sync.dma_start(tables[l][:], xrows[l // 4, l % 4])
+
+        def loadw(g):
+            nc.sync.dma_start(wraw[:, g], wrows[g])
+
+        def look(l, lo, hi):
+            return offsets[:, (l * V + lo) // 16 : (l * V + hi) // 16]
+
+        def move(eng, dst, src):
+            if eng == "s":
+                nc.scalar.copy(dst, src)
+            elif eng == "g":
+                nc.gpsimd.tensor_scalar(dst, src, 1.0, 0.0, MULT, ADD)
+            else:
+                nc.vector.tensor_copy(dst, src)
+
+        def ga(l, lo=0, hi=V):
+            nc.vector.tensor_copy(g4[l // 4][:, l % 4, lo:hi], tables[l][:].indirect(look(l, lo, hi)))
+
+        def gb(l, lo=0, hi=V):
+            nc.vector.tensor_copy(grouped[l // 4][:, lo:hi, l % 4], tables[l][:].indirect(look(l, lo, hi)))
+
+        def cast(eng, l):
+            win[l] = keep.tile([P, T], BF16, name="win%d" % l)
+            move(eng, win[l][:], tables[l][:])
+
+        def gf(l, lo=0, hi=V):
+            nc.scalar.activation(grouped[l // 4][:, lo:hi, l % 4], win[l][:].indirect(look(l, lo, hi)), COPY)
+
+        def inter(eng, g, lo, hi, t0=0, t1=4):
+            move(eng, grouped[g][:, lo:hi, t0:t1], g4[g][:, t0:t1, lo:hi].rearrange("p t n -> p n t"))
+
+        def q(g, lo=0, hi=V):
+            nc.vector.quantize_mx(out=codes[g][:, lo:hi].bitcast(FP8X4), scales=scales[g][:, lo:hi],
+                                  in_=grouped[g][:, lo:hi, :].rearrange("p n j -> p (n j)"))
+
+        def wcopy(eng, g):
+            move(eng, wg[:, g], wraw[:, g].rearrange("p j m -> p m j"))
+
+        def wq(g):
+            nc.vector.quantize_mx(out=wcodes[:, g].bitcast(FP8X4), scales=wscales[:, g],
+                                  in_=wg[:, g].rearrange("p m j -> p (m j)"))
+
+        def mm(g, bank, lo, hi, start, stop):
+            nc.tensor.matmul_mx(out=banks[bank][:, 0 : hi - lo], lhsT=wcodes[:, g].bitcast(FP8X4), lhsT_scale=wscales[:, g],
+                                rhs=codes[g][:, lo:hi].bitcast(FP8X4), rhs_scale=scales[g][:, lo:hi],
+                                start=start, stop=stop)
+
+        def fin(eng, bank, lo, hi, dma):
+            if eng == "s":
+                nc.scalar.activation(res[:, lo:hi], banks[bank][:, 0 : hi - lo], RELU, bias=bias[:])
+            else:
+                nc.vector.tensor_scalar(res[:, lo:hi], banks[bank][:, 0 : hi - lo], bias[:], 0.0, ADD, MAX)
+            (nc.sync if dma == "y" else nc.scalar).dma_start(out[:, lo:hi], res[:, lo:hi])
+
+        nc.vector.memset(warm[:], 0.0)
+        nc.scalar.activation(warm2[:], warm[:], RELU)
+        nc.scalar.dma_start(bias[:], b)
+        load(0)
+        load(2)
+        load(1)
+        load(3)
+        load(4)
+        load(6)
+        load(5)
+        load(7)
+        loadw(0)
+        loadw(1)
+        cast("g", 0)
+        gf(0)
+        gb(2)
+        cast("g", 1)
+        gf(1)
+        gb(3)
+        cast("g", 4)
+        gf(4)
+        q(0)
+        gb(6)
+        cast("v", 5)
+        gf(5)
+        gb(7, 0, 256)
+        wcopy("g", 0)
+        wq(0)
+        wcopy("s", 1)
+        gb(7, 256, 512)
+        mm(0, 0, 0, 256, True, False)
+        mm(0, 1, 256, 512, True, False)
+        q(1, 0, 256)
+        wq(1)
+        mm(1, 0, 0, 256, False, True)
+        fin("s", 0, 0, 256, "y")
+        q(1, 256, 512)
+        mm(1, 1, 256, 512, False, True)
+        fin("v", 1, 256, 512, "s")

@@ -29,30 +29,29 @@ def tile_picked_grid_lin_relu_sub_l_kernel(tc, xT, w, b, offs, out):
         xrows = xT.rearrange("(g p j) c -> g j p c", g=2, j=4)
         wrows = w.rearrange("(g p j) m -> g p j m", g=2, j=4)
         tables = {}
-        for l in range(D):
-            tables[l] = keep.tile([P, T], F32, name="table%d" % l)
-        wraw = keep.tile([P, 2, 4, N], F32, name="wraw")
-        wg = keep.tile([P, 2, N, 4], BF16, name="wg", align_bytes=64)
-        wcodes = keep.tile([P, 2, N], U32, name="wcodes", align_bytes=64)
-        wscales = keep.tile([P, 2, N], U8, name="wscales", align_bytes=64)
-        g4 = {}
+        wraw = {}
+        wg = {}
+        wcodes = {}
+        wscales = {}
         grouped = {}
         codes = {}
         scales = {}
+        pairs = {}
+        win = {}
         for g in (0, 1):
-            g4[g] = keep.tile([P, 4, V], F32, name="g4_%d" % g)
+            wcodes[g] = keep.tile([P, N], U32, name="wcodes%d" % g, align_bytes=64)
+            wscales[g] = keep.tile([P, N], U8, name="wscales%d" % g, align_bytes=64)
             grouped[g] = keep.tile([P, V, 4], BF16, name="grouped%d" % g, align_bytes=64)
-            codes[g] = keep.tile([P, V], U32, name="codes%d" % g, align_bytes=64)
-            scales[g] = keep.tile([P, V], U8, name="scales%d" % g, align_bytes=64)
         banks = [psum.tile([P, 512], F32, name="bank%d" % c) for c in range(4)]
         res = keep.tile([P, V], F32, name="res")
-        win = {}
 
         def load(l):
+            tables[l] = keep.tile([P, T], F32, name="table%d" % l, align_bytes=64)
             nc.sync.dma_start(tables[l][:], xrows[l // 4, l % 4])
 
         def loadw(g):
-            nc.sync.dma_start(wraw[:, g], wrows[g])
+            wraw[g] = keep.tile([P, 4, N], F32, name="wraw%d" % g, align_bytes=64)
+            nc.sync.dma_start(wraw[g][:], wrows[g])
 
         def look(l, lo, hi):
             return offsets[:, (l * V + lo) // 16 : (l * V + hi) // 16]
@@ -65,37 +64,54 @@ def tile_picked_grid_lin_relu_sub_l_kernel(tc, xT, w, b, offs, out):
             else:
                 nc.vector.tensor_copy(dst, src)
 
-        def ga(l, lo=0, hi=V):
-            nc.vector.tensor_copy(g4[l // 4][:, l % 4, lo:hi], tables[l][:].indirect(look(l, lo, hi)))
+        def pair(l, lo, hi):
+            key = (l // 2, lo, hi)
+            if key not in pairs:
+                pairs[key] = keep.tile([P, 2, hi - lo], BF16, name="pair%d_%d_%d" % key, align_bytes=64)
+            return pairs[key]
+
+        def gc(l, lo=0, hi=V):
+            nc.vector.tensor_copy(pair(l, lo, hi)[:, l % 2, :], tables[l][:].indirect(look(l, lo, hi)))
+
+        def gs(l, lo=0, hi=V):
+            nc.scalar.activation(pair(l, lo, hi)[:, l % 2, :], win[l][:].indirect(look(l, lo, hi)), COPY)
+
+        def weave(eng, l, lo=0, hi=V):
+            t = l % 4
+            move(eng, grouped[l // 4][:, lo:hi, t : t + 2], pair(l, lo, hi)[:].rearrange("p t n -> p n t"))
 
         def gb(l, lo=0, hi=V):
             nc.vector.tensor_copy(grouped[l // 4][:, lo:hi, l % 4], tables[l][:].indirect(look(l, lo, hi)))
 
-        def cast(eng, l):
-            win[l] = keep.tile([P, T], BF16, name="win%d" % l)
-            move(eng, win[l][:], tables[l][:])
+        def cast(eng, l, lo=0, hi=T):
+            if l not in win:
+                win[l] = keep.tile([P, T], BF16, name="win%d" % l, align_bytes=64)
+            move(eng, win[l][:, lo:hi], tables[l][:, lo:hi])
 
         def gf(l, lo=0, hi=V):
             nc.scalar.activation(grouped[l // 4][:, lo:hi, l % 4], win[l][:].indirect(look(l, lo, hi)), COPY)
 
-        def inter(eng, g, lo, hi, t0=0, t1=4):
-            move(eng, grouped[g][:, lo:hi, t0:t1], g4[g][:, t0:t1, lo:hi].rearrange("p t n -> p n t"))
-
-        def q(g, lo=0, hi=V):
-            nc.vector.quantize_mx(out=codes[g][:, lo:hi].bitcast(FP8X4), scales=scales[g][:, lo:hi],
+        def q(g, lo=0, hi=V, slot=None):
+            key = (g, lo, hi)
+            codes[key] = keep.tile([P, hi - lo], U32, name=slot or "codes%d_%d_%d" % key, align_bytes=64)
+            scales[key] = keep.tile([P, hi - lo], U8, name="scales%d_%d_%d" % key, align_bytes=64)
+            nc.vector.quantize_mx(out=codes[key][:].bitcast(FP8X4), scales=scales[key][:],
                                   in_=grouped[g][:, lo:hi, :].rearrange("p n j -> p (n j)"))
 
-        def wcopy(eng, g):
-            move(eng, wg[:, g], wraw[:, g].rearrange("p j m -> p m j"))
+        def wcopy(eng, g, lo=0, hi=N):
+            if g not in wg:
+                wg[g] = keep.tile([P, N, 4], BF16, name="wg%d" % g, align_bytes=64)
+            move(eng, wg[g][:, lo:hi], wraw[g][:, :, lo:hi].rearrange("p j m -> p m j"))
 
         def wq(g):
-            nc.vector.quantize_mx(out=wcodes[:, g].bitcast(FP8X4), scales=wscales[:, g],
-                                  in_=wg[:, g].rearrange("p m j -> p (m j)"))
+            nc.vector.quantize_mx(out=wcodes[g][:].bitcast(FP8X4), scales=wscales[g][:],
+                                  in_=wg[g][:].rearrange("p m j -> p (m j)"))
 
-        def mm(g, bank, lo, hi, start, stop):
-            nc.tensor.matmul_mx(out=banks[bank][:, 0 : hi - lo], lhsT=wcodes[:, g].bitcast(FP8X4), lhsT_scale=wscales[:, g],
-                                rhs=codes[g][:, lo:hi].bitcast(FP8X4), rhs_scale=scales[g][:, lo:hi],
-                                start=start, stop=stop)
+        def mm(key, bank, lo, hi, start, stop):
+            g, first = key[0], key[1]
+            nc.tensor.matmul_mx(out=banks[bank][:, 0 : hi - lo], lhsT=wcodes[g][:].bitcast(FP8X4), lhsT_scale=wscales[g][:],
+                                rhs=codes[key][:, lo - first : hi - first].bitcast(FP8X4),
+                                rhs_scale=scales[key][:, lo - first : hi - first], start=start, stop=stop)
 
         def fin(eng, bank, lo, hi, dma):
             if eng == "s":
@@ -106,7 +122,6 @@ def tile_picked_grid_lin_relu_sub_l_kernel(tc, xT, w, b, offs, out):
 
         nc.vector.memset(warm[:], 0.0)
         nc.scalar.activation(warm2[:], warm[:], RELU)
-        nc.scalar.dma_start(bias[:], b)
         load(0)
         load(2)
         load(1)
@@ -117,29 +132,35 @@ def tile_picked_grid_lin_relu_sub_l_kernel(tc, xT, w, b, offs, out):
         load(7)
         loadw(0)
         loadw(1)
-        cast("g", 0)
+        nc.sync.dma_start(bias[:], b)
+        cast("v", 0)
         gf(0)
         gb(2)
-        cast("g", 1)
+        cast("v", 1)
         gf(1)
         gb(3)
-        cast("g", 4)
+        cast("v", 4)
         gf(4)
-        q(0)
+        q(0, slot="table4")
         gb(6)
         cast("v", 5)
-        gf(5)
+        gf(5, 0, 256)
+        gf(5, 256, 512)
         gb(7, 0, 256)
-        wcopy("g", 0)
-        wq(0)
-        wcopy("s", 1)
         gb(7, 256, 512)
-        mm(0, 0, 0, 256, True, False)
-        mm(0, 1, 256, 512, True, False)
+        wcopy("g", 0)
+        wcopy("s", 1)
         q(1, 0, 256)
+        wq(0)
+        mm((0, 0, 512), 0, 0, 256, True, False)
+        mm((0, 0, 512), 1, 256, 384, True, False)
+        mm((0, 0, 512), 2, 384, 512, True, False)
+        q(1, 256, 384, slot="wg0")
         wq(1)
-        mm(1, 0, 0, 256, False, True)
+        mm((1, 0, 256), 0, 0, 256, False, True)
         fin("s", 0, 0, 256, "y")
-        q(1, 256, 512)
-        mm(1, 1, 256, 512, False, True)
-        fin("v", 1, 256, 512, "s")
+        mm((1, 256, 384), 1, 256, 384, False, True)
+        fin("s", 1, 256, 384, "y")
+        q(1, 384, 512, slot="wg1")
+        mm((1, 384, 512), 2, 384, 512, False, True)
+        fin("v", 2, 384, 512, "s")

@@ -122,6 +122,7 @@ def tile_picked_grid_lin_relu_sub_l_kernel(tc, xT, w, b, offs, out):
 
         nc.vector.memset(warm[:], 0.0)
         nc.scalar.activation(warm2[:], warm[:], RELU)
+        nc.scalar.dma_start(bias[:], b)
         load(0)
         load(2)
         load(1)
@@ -132,7 +133,6 @@ def tile_picked_grid_lin_relu_sub_l_kernel(tc, xT, w, b, offs, out):
         load(7)
         loadw(0)
         loadw(1)
-        nc.sync.dma_start(bias[:], b)
         cast("v", 0)
         gf(0)
         gb(2)
@@ -143,24 +143,20 @@ def tile_picked_grid_lin_relu_sub_l_kernel(tc, xT, w, b, offs, out):
         gf(4)
         q(0, slot="table4")
         gb(6)
-        cast("v", 5)
+        cast("g", 5)
         gf(5, 0, 256)
         gf(5, 256, 512)
         gb(7, 0, 256)
         gb(7, 256, 512)
         wcopy("g", 0)
-        wcopy("s", 1)
         q(1, 0, 256)
+        wcopy("v", 1)
         wq(0)
         mm((0, 0, 512), 0, 0, 256, True, False)
-        mm((0, 0, 512), 1, 256, 384, True, False)
-        mm((0, 0, 512), 2, 384, 512, True, False)
-        q(1, 256, 384, slot="wg0")
+        mm((0, 0, 512), 1, 256, 512, True, False)
         wq(1)
         mm((1, 0, 256), 0, 0, 256, False, True)
         fin("s", 0, 0, 256, "y")
-        mm((1, 256, 384), 1, 256, 384, False, True)
-        fin("s", 1, 256, 384, "y")
-        q(1, 384, 512, slot="wg1")
-        mm((1, 384, 512), 2, 384, 512, False, True)
-        fin("v", 2, 384, 512, "s")
+        q(1, 256, 512, slot="wg1")
+        mm((1, 256, 512), 1, 256, 512, False, True)
+        fin("v", 1, 256, 512, "s")

@@ -101,7 +101,11 @@ def tile_picked_grid_lin_relu_sub_l_kernel(tc, xT, w, b, offs, out):
         def wcopy(eng, g, lo=0, hi=N):
             if g not in wg:
                 wg[g] = keep.tile([P, N, 4], BF16, name="wg%d" % g, align_bytes=64)
-            move(eng, wg[g][:, lo:hi], wraw[g][:, :, lo:hi].rearrange("p j m -> p m j"))
+            if eng == "g":
+                move(eng, wg[g][:, lo:hi], wraw[g][:, :, lo:hi].rearrange("p j m -> p m j"))
+            else:
+                move(eng, wg[g][:, lo:hi].rearrange("p (c i) j -> p c j i", i=4),
+                     wraw[g][:, :, lo:hi].rearrange("p j (c i) -> p c j i", i=4))
 
         def wq(g):
             nc.vector.quantize_mx(out=wcodes[g][:].bitcast(FP8X4), scales=wscales[g][:],
@@ -113,11 +117,13 @@ def tile_picked_grid_lin_relu_sub_l_kernel(tc, xT, w, b, offs, out):
                                 rhs=codes[key][:, lo - first : hi - first].bitcast(FP8X4),
                                 rhs_scale=scales[key][:, lo - first : hi - first], start=start, stop=stop)
 
-        def fin(eng, bank, lo, hi, dma):
+        def fin(eng, bank, lo, hi):
             if eng == "s":
                 nc.scalar.activation(res[:, lo:hi], banks[bank][:, 0 : hi - lo], RELU, bias=bias[:])
             else:
                 nc.vector.tensor_scalar(res[:, lo:hi], banks[bank][:, 0 : hi - lo], bias[:], 0.0, ADD, MAX)
+
+        def store(dma, lo, hi):
             (nc.sync if dma == "y" else nc.scalar).dma_start(out[:, lo:hi], res[:, lo:hi])
 
         nc.vector.memset(warm[:], 0.0)
@@ -150,13 +156,20 @@ def tile_picked_grid_lin_relu_sub_l_kernel(tc, xT, w, b, offs, out):
         gb(7, 256, 512)
         wcopy("g", 0)
         q(1, 0, 256)
-        wcopy("v", 1)
+        wcopy("s", 1, 0, 64)
+        wcopy("v", 1, 64, 128)
         wq(0)
         mm((0, 0, 512), 0, 0, 256, True, False)
-        mm((0, 0, 512), 1, 256, 512, True, False)
+        mm((0, 0, 512), 1, 256, 384, True, False)
+        mm((0, 0, 512), 2, 384, 512, True, False)
+        q(1, 256, 384, slot="wg0")
         wq(1)
         mm((1, 0, 256), 0, 0, 256, False, True)
-        fin("s", 0, 0, 256, "y")
-        q(1, 256, 512, slot="wg1")
-        mm((1, 256, 512), 1, 256, 512, False, True)
-        fin("v", 1, 256, 512, "s")
+        fin("s", 0, 0, 256)
+        store("s", 0, 256)
+        mm((1, 256, 384), 1, 256, 384, False, True)
+        q(1, 384, 512, slot="wg1")
+        mm((1, 384, 512), 2, 384, 512, False, True)
+        fin("v", 1, 256, 384)
+        fin("v", 2, 384, 512)
+        store("y", 256, 512)

@@ -6,6 +6,7 @@ K, T, D, V, N = 1024, 1024, 8, 512, 128
 FLOPS = 2 * K * N * V
 F32 = mybir.dt.float32
 BF16 = mybir.dt.bfloat16
+I32 = mybir.dt.int32
 U32 = mybir.dt.uint32
 U16 = mybir.dt.uint16
 U8 = mybir.dt.uint8
@@ -41,7 +42,6 @@ def tile_picked_grid_lin_relu_sub_l_kernel(tc, xT, w, b, offs, out):
         for g in (0, 1):
             wcodes[g] = keep.tile([P, N], U32, name="wcodes%d" % g, align_bytes=64)
             wscales[g] = keep.tile([P, N], U8, name="wscales%d" % g, align_bytes=64)
-            grouped[g] = keep.tile([P, V, 4], BF16, name="grouped%d" % g, align_bytes=64)
         banks = [psum.tile([P, 512], F32, name="bank%d" % c) for c in range(4)]
         res = keep.tile([P, V], F32, name="res")
 
@@ -64,39 +64,47 @@ def tile_picked_grid_lin_relu_sub_l_kernel(tc, xT, w, b, offs, out):
             else:
                 nc.vector.tensor_copy(dst, src)
 
-        def pair(l, lo, hi):
-            key = (l // 2, lo, hi)
+        def pair(g, lo, hi):
+            key = (g, lo, hi)
             if key not in pairs:
-                pairs[key] = keep.tile([P, 2, hi - lo], BF16, name="pair%d_%d_%d" % key, align_bytes=64)
+                pairs[key] = keep.tile([P, 2, hi - lo, 2], BF16, name="pair%d_%d_%d" % key, align_bytes=64)
             return pairs[key]
 
-        def gc(l, lo=0, hi=V):
-            nc.vector.tensor_copy(pair(l, lo, hi)[:, l % 2, :], tables[l][:].indirect(look(l, lo, hi)))
+        def group(g, lo, hi):
+            key = (g, lo, hi)
+            if key not in grouped:
+                grouped[key] = keep.tile([P, hi - lo, 4], BF16, name="grouped%d_%d_%d" % key, align_bytes=64)
+            return grouped[key]
+
+        def gv(l, lo=0, hi=V):
+            nc.vector.tensor_copy(pair(l // 4, lo, hi)[:, l % 4 // 2, :, l % 2], tables[l][:].indirect(look(l, lo, hi)))
 
         def gs(l, lo=0, hi=V):
-            nc.scalar.activation(pair(l, lo, hi)[:, l % 2, :], win[l][:].indirect(look(l, lo, hi)), COPY)
-
-        def weave(eng, l, lo=0, hi=V):
-            t = l % 4
-            move(eng, grouped[l // 4][:, lo:hi, t : t + 2], pair(l, lo, hi)[:].rearrange("p t n -> p n t"))
+            nc.scalar.activation(pair(l // 4, lo, hi)[:, l % 4 // 2, :, l % 2], win[l][:].indirect(look(l, lo, hi)), COPY)
 
         def gb(l, lo=0, hi=V):
-            nc.vector.tensor_copy(grouped[l // 4][:, lo:hi, l % 4], tables[l][:].indirect(look(l, lo, hi)))
+            nc.vector.tensor_copy(group(l // 4, lo, hi)[:, :, l % 4], tables[l][:].indirect(look(l, lo, hi)))
+
+        def gf(l, lo=0, hi=V):
+            nc.scalar.activation(group(l // 4, lo, hi)[:, :, l % 4], win[l][:].indirect(look(l, lo, hi)), COPY)
+
+        def weave(eng, key, a, z):
+            word = U32 if eng == "s" else I32
+            src = pair(*key)[:].rearrange("p u n t -> p u (n t)").bitcast(word)
+            dst = group(*key)[:].bitcast(word)
+            move(eng, dst[:, a:z, :], src[:, :, a:z].rearrange("p u n -> p n u"))
 
         def cast(eng, l, lo=0, hi=T):
             if l not in win:
                 win[l] = keep.tile([P, T], BF16, name="win%d" % l, align_bytes=64)
             move(eng, win[l][:, lo:hi], tables[l][:, lo:hi])
 
-        def gf(l, lo=0, hi=V):
-            nc.scalar.activation(grouped[l // 4][:, lo:hi, l % 4], win[l][:].indirect(look(l, lo, hi)), COPY)
-
         def q(g, lo=0, hi=V, slot=None):
             key = (g, lo, hi)
             codes[key] = keep.tile([P, hi - lo], U32, name=slot or "codes%d_%d_%d" % key, align_bytes=64)
             scales[key] = keep.tile([P, hi - lo], U8, name="scales%d_%d_%d" % key, align_bytes=64)
             nc.vector.quantize_mx(out=codes[key][:].bitcast(FP8X4), scales=scales[key][:],
-                                  in_=grouped[g][:, lo:hi, :].rearrange("p n j -> p (n j)"))
+                                  in_=group(g, lo, hi)[:].rearrange("p n j -> p (n j)"))
 
         def wcopy(eng, g, lo=0, hi=N):
             if g not in wg:
@@ -129,46 +137,44 @@ def tile_picked_grid_lin_relu_sub_l_kernel(tc, xT, w, b, offs, out):
         nc.vector.memset(warm[:], 0.0)
         nc.scalar.activation(warm2[:], warm[:], RELU)
         nc.scalar.dma_start(bias[:], b)
-        load(0)
-        load(2)
-        load(1)
-        load(3)
-        load(4)
-        load(6)
-        load(5)
-        load(7)
+        pieces = ((0, 256), (256, 384), (384, 512))
         loadw(0)
+        for l in (0, 2, 1, 3, 4, 6, 5, 7):
+            load(l)
         loadw(1)
-        cast("v", 0)
-        gf(0)
-        gb(2)
-        cast("v", 1)
-        gf(1)
-        gb(3)
-        cast("v", 4)
-        gf(4)
-        q(0, slot="table4")
-        gb(6)
-        cast("g", 5)
-        gf(5, 0, 256)
-        gf(5, 256, 512)
-        gb(7, 0, 256)
-        gb(7, 256, 512)
-        wcopy("g", 0)
-        q(1, 0, 256)
-        wcopy("s", 1, 0, 64)
-        wcopy("v", 1, 64, 128)
+        wcopy("s", 0)
         wq(0)
-        mm((0, 0, 512), 0, 0, 256, True, False)
-        mm((0, 0, 512), 1, 256, 384, True, False)
-        mm((0, 0, 512), 2, 384, 512, True, False)
-        q(1, 256, 384, slot="wg0")
+        cast("v", 0)
+        gs(0)
+        gv(2)
+        cast("v", 1)
+        gs(1)
+        gv(3)
+        cast("v", 4)
+        weave("s", (0, 0, V), 0, 512)
+        for lo, hi in pieces:
+            gs(4, lo, hi)
+        for lo, hi in pieces:
+            gv(6, lo, hi)
+        cast("v", 5)
+        q(0, slot="table5")
+        for c, (lo, hi) in enumerate(pieces):
+            mm((0, 0, V), c, lo, hi, True, False)
+        for lo, hi in pieces:
+            gs(5, lo, hi)
+        for lo, hi in pieces:
+            gv(7, lo, hi)
+        for lo, hi in pieces:
+            weave("s", (1, lo, hi), 0, hi - lo)
+        wcopy("g", 1)
+        q(1, 0, 256)
         wq(1)
         mm((1, 0, 256), 0, 0, 256, False, True)
+        q(1, 256, 384, slot="wg1")
+        q(1, 384, 512)
         fin("s", 0, 0, 256)
         store("s", 0, 256)
         mm((1, 256, 384), 1, 256, 384, False, True)
-        q(1, 384, 512, slot="wg1")
         mm((1, 384, 512), 2, 384, 512, False, True)
         fin("v", 1, 256, 384)
         fin("v", 2, 384, 512)

@@ -64,23 +64,26 @@ def tile_picked_grid_lin_relu_sub_l_kernel(tc, xT, w, b, offs, out):
             else:
                 nc.vector.tensor_copy(dst, src)
 
-        def pair(g, lo, hi):
-            key = (g, lo, hi)
-            if key not in pairs:
-                pairs[key] = keep.tile([P, 2, hi - lo, 2], BF16, name="pair%d_%d_%d" % key, align_bytes=64)
-            return pairs[key]
+        def pair(g):
+            if g not in pairs:
+                pairs[g] = keep.tile([P, 4 * V], BF16, name="pair%d" % g, align_bytes=64)
+            return pairs[g]
 
-        def group(g, lo, hi):
+        def place(l, lo, hi):
+            first = l % 4 // 2 * 2 * V + l % 2
+            return pair(l // 4)[:, first + 2 * lo : first + 2 * hi - 1 : 2]
+
+        def group(g, lo, hi, slot=None):
             key = (g, lo, hi)
             if key not in grouped:
-                grouped[key] = keep.tile([P, hi - lo, 4], BF16, name="grouped%d_%d_%d" % key, align_bytes=64)
+                grouped[key] = keep.tile([P, hi - lo, 4], BF16, name=slot or "grouped%d_%d_%d" % key, align_bytes=64)
             return grouped[key]
 
         def gv(l, lo=0, hi=V):
-            nc.vector.tensor_copy(pair(l // 4, lo, hi)[:, l % 4 // 2, :, l % 2], tables[l][:].indirect(look(l, lo, hi)))
+            nc.vector.tensor_copy(place(l, lo, hi), tables[l][:].indirect(look(l, lo, hi)))
 
         def gs(l, lo=0, hi=V):
-            nc.scalar.activation(pair(l // 4, lo, hi)[:, l % 4 // 2, :, l % 2], win[l][:].indirect(look(l, lo, hi)), COPY)
+            nc.scalar.activation(place(l, lo, hi), win[l][:].indirect(look(l, lo, hi)), COPY)
 
         def gb(l, lo=0, hi=V):
             nc.vector.tensor_copy(group(l // 4, lo, hi)[:, :, l % 4], tables[l][:].indirect(look(l, lo, hi)))
@@ -88,23 +91,28 @@ def tile_picked_grid_lin_relu_sub_l_kernel(tc, xT, w, b, offs, out):
         def gf(l, lo=0, hi=V):
             nc.scalar.activation(group(l // 4, lo, hi)[:, :, l % 4], win[l][:].indirect(look(l, lo, hi)), COPY)
 
-        def weave(eng, key, a, z):
-            word = U32 if eng == "s" else I32
-            src = pair(*key)[:].rearrange("p u n t -> p u (n t)").bitcast(word)
-            dst = group(*key)[:].bitcast(word)
-            move(eng, dst[:, a:z, :], src[:, :, a:z].rearrange("p u n -> p n u"))
+        def weave(eng, g, lo, hi):
+            word = I32 if eng == "v" else U32
+            src = pair(g)[:].bitcast(word).rearrange("p (u n) -> p n u", u=2)
+            move(eng, group(g, lo, hi)[:].bitcast(word), src[:, lo:hi, :])
 
         def cast(eng, l, lo=0, hi=T):
             if l not in win:
                 win[l] = keep.tile([P, T], BF16, name="win%d" % l, align_bytes=64)
             move(eng, win[l][:, lo:hi], tables[l][:, lo:hi])
 
-        def q(g, lo=0, hi=V, slot=None):
+        def code_tiles(g, lo, hi, slot=None):
             key = (g, lo, hi)
             codes[key] = keep.tile([P, hi - lo], U32, name=slot or "codes%d_%d_%d" % key, align_bytes=64)
             scales[key] = keep.tile([P, hi - lo], U8, name="scales%d_%d_%d" % key, align_bytes=64)
-            nc.vector.quantize_mx(out=codes[key][:].bitcast(FP8X4), scales=scales[key][:],
-                                  in_=group(g, lo, hi)[:].rearrange("p n j -> p (n j)"))
+
+        def q(key, lo, hi):
+            first = key[1]
+            if key not in codes:
+                code_tiles(*key)
+            nc.vector.quantize_mx(out=codes[key][:, lo - first : hi - first].bitcast(FP8X4),
+                                  scales=scales[key][:, lo - first : hi - first],
+                                  in_=group(key[0], lo, hi)[:].rearrange("p n j -> p (n j)"))
 
         def wcopy(eng, g, lo=0, hi=N):
             if g not in wg:
@@ -137,9 +145,9 @@ def tile_picked_grid_lin_relu_sub_l_kernel(tc, xT, w, b, offs, out):
         nc.vector.memset(warm[:], 0.0)
         nc.scalar.activation(warm2[:], warm[:], RELU)
         nc.scalar.dma_start(bias[:], b)
-        pieces = ((0, 256), (256, 384), (384, 512))
+        pieces = ((0, 128), (128, 256), (256, 384), (384, 512))
         loadw(0)
-        for l in (0, 2, 1, 3, 4, 6, 5, 7):
+        for l in (0, 2, 1, 3, 4, 5, 6, 7):
             load(l)
         loadw(1)
         wcopy("s", 0)
@@ -151,31 +159,30 @@ def tile_picked_grid_lin_relu_sub_l_kernel(tc, xT, w, b, offs, out):
         gs(1)
         gv(3)
         cast("v", 4)
-        weave("s", (0, 0, V), 0, 512)
-        for lo, hi in pieces:
-            gs(4, lo, hi)
-        for lo, hi in pieces:
-            gv(6, lo, hi)
+        weave("s", 0, 0, 256)
+        weave("s", 0, 256, 512)
+        gs(4)
         cast("v", 5)
-        q(0, slot="table5")
+        code_tiles(0, 0, V, slot="table4")
+        q((0, 0, V), 0, 256)
+        q((0, 0, V), 256, 512)
         for c, (lo, hi) in enumerate(pieces):
             mm((0, 0, V), c, lo, hi, True, False)
-        for lo, hi in pieces:
-            gs(5, lo, hi)
+        gs(5)
+        gv(6)
         for lo, hi in pieces:
             gv(7, lo, hi)
         for lo, hi in pieces:
-            weave("s", (1, lo, hi), 0, hi - lo)
+            weave("s", 1, lo, hi)
         wcopy("g", 1)
-        q(1, 0, 256)
         wq(1)
-        mm((1, 0, 256), 0, 0, 256, False, True)
-        q(1, 256, 384, slot="wg1")
-        q(1, 384, 512)
-        fin("s", 0, 0, 256)
-        store("s", 0, 256)
-        mm((1, 256, 384), 1, 256, 384, False, True)
-        mm((1, 384, 512), 2, 384, 512, False, True)
-        fin("v", 1, 256, 384)
-        fin("v", 2, 384, 512)
+        code_tiles(1, 0, V, slot="wraw1")
+        for c, (lo, hi) in enumerate(pieces):
+            q((1, 0, V), lo, hi)
+            mm((1, 0, V), c, lo, hi, False, True)
+        fin("s", 0, 0, 128)
+        fin("v", 1, 128, 256)
+        store("y", 0, 256)
+        fin("s", 2, 256, 384)
+        fin("v", 3, 384, 512)
         store("y", 256, 512)

@@ -49,6 +49,16 @@ def tile_picked_grid_lin_relu_sub_l_kernel(tc, xT, w, b, offs, out):
             tables[l] = keep.tile([P, T], F32, name="table%d" % l, align_bytes=64)
             nc.sync.dma_start(tables[l][:], xrows[l // 4, l % 4])
 
+        def load_halves(l):
+            for h in (0, 1):
+                tables[l, h] = keep.tile([P, T // 2], F32, name="table%d_%d" % (l, h), align_bytes=64)
+                nc.sync.dma_start(tables[l, h][:], xrows[l // 4, l % 4][:, h * T // 2 : (h + 1) * T // 2])
+
+        def cast_half(eng, l, h):
+            if l not in win:
+                win[l] = keep.tile([P, T], BF16, name="win%d" % l, align_bytes=64)
+            move(eng, win[l][:, h * T // 2 : (h + 1) * T // 2], tables[l, h][:])
+
         def loadw(g):
             wraw[g] = keep.tile([P, 4, N], F32, name="wraw%d" % g, align_bytes=64)
             nc.sync.dma_start(wraw[g][:], wrows[g])
@@ -147,29 +157,34 @@ def tile_picked_grid_lin_relu_sub_l_kernel(tc, xT, w, b, offs, out):
         nc.scalar.dma_start(bias[:], b)
         pieces = ((0, 128), (128, 256), (256, 384), (384, 512))
         loadw(0)
-        for l in (0, 2, 1, 3, 4, 5, 6, 7):
-            load(l)
+        for l in range(D):
+            (load_halves if l == 5 else load)(l)
         loadw(1)
         wcopy("s", 0)
         wq(0)
         cast("v", 0)
         gs(0)
-        gv(2)
         cast("v", 1)
         gs(1)
-        gv(3)
+        gv(2, 0, 256)
+        gv(2, 256, 512)
+        gv(3, 0, 256)
+        gv(3, 256, 512)
         cast("v", 4)
         weave("s", 0, 0, 256)
         weave("s", 0, 256, 512)
         gs(4)
-        cast("v", 5)
-        code_tiles(0, 0, V, slot="table4")
-        q((0, 0, V), 0, 256)
-        q((0, 0, V), 256, 512)
+        cast_half("v", 5, 0)
+        code_tiles(0, 0, 256, slot="table4")
+        q((0, 0, 256), 0, 256)
+        cast_half("v", 5, 1)
+        code_tiles(0, 256, 512, slot="table5_0")
+        q((0, 256, 512), 256, 512)
         for c, (lo, hi) in enumerate(pieces):
-            mm((0, 0, V), c, lo, hi, True, False)
+            mm((0, lo // 256 * 256, lo // 256 * 256 + 256), c, lo, hi, True, False)
         gs(5)
-        gv(6)
+        gv(6, 0, 256)
+        gv(6, 256, 512)
         for lo, hi in pieces:
             gv(7, lo, hi)
         for lo, hi in pieces:

@@ -154,20 +154,19 @@ def tile_picked_grid_lin_relu_sub_l_kernel(tc, xT, w, b, offs, out):
 
         nc.vector.memset(warm[:], 0.0)
         nc.scalar.activation(warm2[:], warm[:], RELU)
-        nc.scalar.dma_start(bias[:], b)
         pieces = ((0, 128), (128, 256), (256, 384), (384, 512))
         loadw(0)
-        for l in range(D):
+        for l in (0, 2, 1, 3, 4, 5, 6, 7):
             (load_halves if l == 5 else load)(l)
         loadw(1)
+        nc.sync.dma_start(bias[:], b)
         wcopy("s", 0)
         wq(0)
         cast("v", 0)
         gs(0)
+        gv(2)
         cast("v", 1)
         gs(1)
-        gv(2, 0, 256)
-        gv(2, 256, 512)
         gv(3, 0, 256)
         gv(3, 256, 512)
         cast("v", 4)
@@ -183,21 +182,23 @@ def tile_picked_grid_lin_relu_sub_l_kernel(tc, xT, w, b, offs, out):
         for c, (lo, hi) in enumerate(pieces):
             mm((0, lo // 256 * 256, lo // 256 * 256 + 256), c, lo, hi, True, False)
         gs(5)
-        gv(6, 0, 256)
-        gv(6, 256, 512)
+        gv(6)
         for lo, hi in pieces:
             gv(7, lo, hi)
         for lo, hi in pieces:
             weave("s", 1, lo, hi)
         wcopy("g", 1)
+        q((1, 0, 128), 0, 128)
         wq(1)
-        code_tiles(1, 0, V, slot="wraw1")
-        for c, (lo, hi) in enumerate(pieces):
-            q((1, 0, V), lo, hi)
-            mm((1, 0, V), c, lo, hi, False, True)
+        mm((1, 0, 128), 0, 0, 128, False, True)
+        code_tiles(1, 128, V, slot="wraw1")
+        for c, (lo, hi) in enumerate(pieces[1:]):
+            q((1, 128, V), lo, hi)
+            mm((1, 128, V), c + 1, lo, hi, False, True)
         fin("s", 0, 0, 128)
         fin("v", 1, 128, 256)
         store("y", 0, 256)
         fin("s", 2, 256, 384)
+        store("s", 256, 384)
         fin("v", 3, 384, 512)
-        store("y", 256, 512)
+        store("y", 384, 512)

@@ -133,6 +133,16 @@ def tile_picked_grid_lin_relu_sub_l_kernel(tc, xT, w, b, offs, out):
                 move(eng, wg[g][:, lo:hi].rearrange("p (c i) j -> p c j i", i=4),
                      wraw[g][:, :, lo:hi].rearrange("p j (c i) -> p c j i", i=4))
 
+        def loadw_halves(g):
+            for h in (0, 1):
+                wraw[g, h] = keep.tile([P, 2, N], F32, name="wraw%d_%d" % (g, h), align_bytes=64)
+                nc.sync.dma_start(wraw[g, h][:], wrows[g][:, 2 * h : 2 * h + 2, :])
+
+        def wcopy_half(eng, g, h):
+            if g not in wg:
+                wg[g] = keep.tile([P, N, 4], BF16, name="wg%d" % g, align_bytes=64)
+            move(eng, wg[g][:, :, 2 * h : 2 * h + 2], wraw[g, h][:].rearrange("p j m -> p m j"))
+
         def wq(g):
             nc.vector.quantize_mx(out=wcodes[g][:].bitcast(FP8X4), scales=wscales[g][:],
                                   in_=wg[g][:].rearrange("p m j -> p (m j)"))
@@ -174,13 +184,12 @@ def tile_picked_grid_lin_relu_sub_l_kernel(tc, xT, w, b, offs, out):
         weave("s", 0, 256, 512)
         gs(4)
         cast_half("v", 5, 0)
-        code_tiles(0, 0, 256, slot="table4")
-        q((0, 0, 256), 0, 256)
         cast_half("v", 5, 1)
-        code_tiles(0, 256, 512, slot="table5_0")
-        q((0, 256, 512), 256, 512)
+        code_tiles(0, 0, V, slot="table5_0")
+        q((0, 0, V), 0, 256)
+        q((0, 0, V), 256, 512)
         for c, (lo, hi) in enumerate(pieces):
-            mm((0, lo // 256 * 256, lo // 256 * 256 + 256), c, lo, hi, True, False)
+            mm((0, 0, V), c, lo, hi, True, False)
         gs(5)
         gv(6)
         for lo, hi in pieces:
@@ -196,9 +205,9 @@ def tile_picked_grid_lin_relu_sub_l_kernel(tc, xT, w, b, offs, out):
             q((1, 128, V), lo, hi)
             mm((1, 128, V), c + 1, lo, hi, False, True)
         fin("s", 0, 0, 128)
-        fin("v", 1, 128, 256)
+        fin("s", 1, 128, 256)
         store("y", 0, 256)
         fin("s", 2, 256, 384)
-        store("s", 256, 384)
+        store("y", 256, 384)
         fin("v", 3, 384, 512)
         store("y", 384, 512)

@@ -45,9 +45,9 @@ def tile_picked_grid_lin_relu_sub_l_kernel(tc, xT, w, b, offs, out):
         banks = [psum.tile([P, 512], F32, name="bank%d" % c) for c in range(4)]
         res = keep.tile([P, V], F32, name="res")
 
-        def load(l):
+        def load(l, queue=nc.sync):
             tables[l] = keep.tile([P, T], F32, name="table%d" % l, align_bytes=64)
-            nc.sync.dma_start(tables[l][:], xrows[l // 4, l % 4])
+            queue.dma_start(tables[l][:], xrows[l // 4, l % 4])
 
         def load_halves(l):
             for h in (0, 1):
@@ -59,9 +59,9 @@ def tile_picked_grid_lin_relu_sub_l_kernel(tc, xT, w, b, offs, out):
                 win[l] = keep.tile([P, T], BF16, name="win%d" % l, align_bytes=64)
             move(eng, win[l][:, h * T // 2 : (h + 1) * T // 2], tables[l, h][:])
 
-        def loadw(g):
+        def loadw(g, queue=nc.sync):
             wraw[g] = keep.tile([P, 4, N], F32, name="wraw%d" % g, align_bytes=64)
-            nc.sync.dma_start(wraw[g][:], wrows[g])
+            queue.dma_start(wraw[g][:], wrows[g])
 
         def look(l, lo, hi):
             return offsets[:, (l * V + lo) // 16 : (l * V + hi) // 16]
@@ -162,11 +162,12 @@ def tile_picked_grid_lin_relu_sub_l_kernel(tc, xT, w, b, offs, out):
         def store(dma, lo, hi):
             (nc.sync if dma == "y" else nc.scalar).dma_start(out[:, lo:hi], res[:, lo:hi])
 
+        loadw(0, nc.scalar)
+        load(1, nc.scalar)
         nc.vector.memset(warm[:], 0.0)
         nc.scalar.activation(warm2[:], warm[:], RELU)
         pieces = ((0, 128), (128, 256), (256, 384), (384, 512))
-        loadw(0)
-        for l in (0, 2, 1, 3, 4, 5, 6, 7):
+        for l in (0, 2, 3, 4, 5, 6, 7):
             (load_halves if l == 5 else load)(l)
         loadw(1)
         nc.sync.dma_start(bias[:], b)
@@ -174,9 +175,9 @@ def tile_picked_grid_lin_relu_sub_l_kernel(tc, xT, w, b, offs, out):
         wq(0)
         cast("v", 0)
         gs(0)
-        gv(2)
         cast("v", 1)
         gs(1)
+        gv(2)
         gv(3, 0, 256)
         gv(3, 256, 512)
         cast("v", 4)

@@ -2,11 +2,16 @@ from contextlib import ExitStack
 
 import concourse.mybir as mybir
 
-K, T, D, V, N = 1024, 1024, 8, 512, 128
+K, T, V, N = 1024, 1024, 512, 128
+LEVELS = 8
 FLOPS = 2 * K * N * V
+P = 128
+PACK = 4
+STRIPE = 16
+HALF = V // 2
+PIECE = 128
 F32 = mybir.dt.float32
 BF16 = mybir.dt.bfloat16
-I32 = mybir.dt.int32
 U32 = mybir.dt.uint32
 U16 = mybir.dt.uint16
 U8 = mybir.dt.uint8
@@ -14,7 +19,6 @@ FP8X4 = mybir.dt.float8_e4m3fn_x4
 COPY = mybir.ActivationFunctionType.Copy
 RELU = mybir.ActivationFunctionType.Relu
 MULT, ADD, MAX = mybir.AluOpType.mult, mybir.AluOpType.add, mybir.AluOpType.max
-P = 128
 
 
 def tile_picked_grid_lin_relu_sub_l_kernel(tc, xT, w, b, offs, out):
@@ -22,193 +26,145 @@ def tile_picked_grid_lin_relu_sub_l_kernel(tc, xT, w, b, offs, out):
     with ExitStack() as ctx:
         keep = ctx.enter_context(tc.tile_pool(name="keep", bufs=1))
         psum = ctx.enter_context(tc.psum_pool(name="psum", bufs=1))
-        offsets = keep.tile([P, D * V // 16], U16, name="offsets")
+
+        def sbuf(shape, dtype, tag):
+            return keep.tile(shape, dtype, name=tag, align_bytes=64)
+
+        offsets = keep.tile([P, LEVELS * V // STRIPE], U16, name="offsets")
         nc.sync.dma_start(offsets[:], offs)
         bias = keep.tile([P, 1], F32, name="bias")
-        warm = keep.tile([P, 1], F32, name="warm")
-        warm2 = keep.tile([P, 1], F32, name="warm2")
-        xrows = xT.rearrange("(g p j) c -> g j p c", g=2, j=4)
-        wrows = w.rearrange("(g p j) m -> g p j m", g=2, j=4)
-        tables = {}
-        wraw = {}
-        wg = {}
-        wcodes = {}
-        wscales = {}
-        grouped = {}
-        codes = {}
-        scales = {}
-        pairs = {}
-        win = {}
+        x_rows = xT.rearrange("(g p t) c -> g t p c", g=2, t=PACK)
+        w_rows = w.rearrange("(g p t) m -> g p t m", g=2, t=PACK)
+        w_codes = {}
+        w_scales = {}
         for g in (0, 1):
-            wcodes[g] = keep.tile([P, N], U32, name="wcodes%d" % g, align_bytes=64)
-            wscales[g] = keep.tile([P, N], U8, name="wscales%d" % g, align_bytes=64)
-        banks = [psum.tile([P, 512], F32, name="bank%d" % c) for c in range(4)]
-        res = keep.tile([P, V], F32, name="res")
+            w_codes[g] = sbuf([P, N], U32, "w_codes%d" % g)
+            w_scales[g] = sbuf([P, N], U8, "w_scales%d" % g)
+        pieces = [(lo, lo + PIECE) for lo in range(0, V, PIECE)]
+        banks = {lo: psum.tile([P, 512], F32, name="bank%d" % lo) for lo, hi in pieces}
+        result = keep.tile([P, V], F32, name="result")
 
-        def load(l, queue=nc.sync):
-            tables[l] = keep.tile([P, T], F32, name="table%d" % l, align_bytes=64)
-            queue.dma_start(tables[l][:], xrows[l // 4, l % 4])
+        def load_table(level, queue, lo=0, hi=T):
+            table = sbuf([P, hi - lo], F32, "table%d_%d" % (level, lo))
+            queue.dma_start(table[:], x_rows[level // PACK, level % PACK][:, lo:hi])
+            return table
 
-        def load_halves(l):
-            for h in (0, 1):
-                tables[l, h] = keep.tile([P, T // 2], F32, name="table%d_%d" % (l, h), align_bytes=64)
-                nc.sync.dma_start(tables[l, h][:], xrows[l // 4, l % 4][:, h * T // 2 : (h + 1) * T // 2])
+        def load_weights(g, queue):
+            raw = sbuf([P, PACK, N], F32, "w_raw%d" % g)
+            queue.dma_start(raw[:], w_rows[g])
+            return raw
 
-        def cast_half(eng, l, h):
-            if l not in win:
-                win[l] = keep.tile([P, T], BF16, name="win%d" % l, align_bytes=64)
-            move(eng, win[l][:, h * T // 2 : (h + 1) * T // 2], tables[l, h][:])
+        def entries(level, lo, hi):
+            return offsets[:, (level * V + lo) // STRIPE : (level * V + hi) // STRIPE]
 
-        def loadw(g, queue=nc.sync):
-            wraw[g] = keep.tile([P, 4, N], F32, name="wraw%d" % g, align_bytes=64)
-            queue.dma_start(wraw[g][:], wrows[g])
+        def pair_places(pairs, level, lo, hi):
+            first = level % PACK // 2 * 2 * V + level % 2
+            return pairs[:, first + 2 * lo : first + 2 * hi - 1 : 2]
 
-        def look(l, lo, hi):
-            return offsets[:, (l * V + lo) // 16 : (l * V + hi) // 16]
+        def look_up_vector(pairs, table, level, lo=0, hi=V):
+            nc.vector.tensor_copy(pair_places(pairs, level, lo, hi), table[:].indirect(entries(level, lo, hi)))
 
-        def move(eng, dst, src):
-            if eng == "s":
-                nc.scalar.copy(dst, src)
-            elif eng == "g":
-                nc.gpsimd.tensor_scalar(dst, src, 1.0, 0.0, MULT, ADD)
-            else:
-                nc.vector.tensor_copy(dst, src)
+        def look_up_scalar(pairs, rounded, level):
+            nc.scalar.activation(pair_places(pairs, level, 0, V), rounded[:].indirect(entries(level, 0, V)), COPY)
 
-        def pair(g):
-            if g not in pairs:
-                pairs[g] = keep.tile([P, 4 * V], BF16, name="pair%d" % g, align_bytes=64)
-            return pairs[g]
+        def round_table(level, table):
+            rounded = sbuf([P, T], BF16, "rounded%d" % level)
+            nc.vector.tensor_copy(rounded[:], table[:])
+            return rounded
 
-        def place(l, lo, hi):
-            first = l % 4 // 2 * 2 * V + l % 2
-            return pair(l // 4)[:, first + 2 * lo : first + 2 * hi - 1 : 2]
+        def weave(pairs, g, lo, hi):
+            words = pairs[:].bitcast(U32).rearrange("p (u v) -> p v u", u=2)
+            woven = sbuf([P, hi - lo, PACK], BF16, "woven%d_%d" % (g, lo))
+            nc.scalar.copy(woven[:].bitcast(U32), words[:, lo:hi, :])
+            return woven
 
-        def group(g, lo, hi, slot=None):
-            key = (g, lo, hi)
-            if key not in grouped:
-                grouped[key] = keep.tile([P, hi - lo, 4], BF16, name=slot or "grouped%d_%d_%d" % key, align_bytes=64)
-            return grouped[key]
+        def code_tiles(g, lo, hi, tag):
+            return sbuf([P, hi - lo], U32, tag), sbuf([P, hi - lo], U8, "x_scales%d_%d" % (g, lo)), lo
 
-        def gv(l, lo=0, hi=V):
-            nc.vector.tensor_copy(place(l, lo, hi), tables[l][:].indirect(look(l, lo, hi)))
+        def quantise_points(tiles, woven, lo, hi):
+            codes, scales, first = tiles
+            nc.vector.quantize_mx(out=codes[:, lo - first : hi - first].bitcast(FP8X4),
+                                  scales=scales[:, lo - first : hi - first],
+                                  in_=woven[:].rearrange("p v t -> p (v t)"))
 
-        def gs(l, lo=0, hi=V):
-            nc.scalar.activation(place(l, lo, hi), win[l][:].indirect(look(l, lo, hi)), COPY)
+        def quantise_weights(g, grouped):
+            nc.vector.quantize_mx(out=w_codes[g][:].bitcast(FP8X4), scales=w_scales[g][:],
+                                  in_=grouped[:].rearrange("p m t -> p (m t)"))
 
-        def gb(l, lo=0, hi=V):
-            nc.vector.tensor_copy(group(l // 4, lo, hi)[:, :, l % 4], tables[l][:].indirect(look(l, lo, hi)))
+        def multiply(g, tiles, lo, hi):
+            codes, scales, first = tiles
+            nc.tensor.matmul_mx(out=banks[lo][:, 0 : hi - lo], lhsT=w_codes[g][:].bitcast(FP8X4), lhsT_scale=w_scales[g][:],
+                                rhs=codes[:, lo - first : hi - first].bitcast(FP8X4),
+                                rhs_scale=scales[:, lo - first : hi - first], start=g == 0, stop=g == 1)
 
-        def gf(l, lo=0, hi=V):
-            nc.scalar.activation(group(l // 4, lo, hi)[:, :, l % 4], win[l][:].indirect(look(l, lo, hi)), COPY)
+        def finish_scalar(lo, hi):
+            nc.scalar.activation(result[:, lo:hi], banks[lo][:, 0 : hi - lo], RELU, bias=bias[:])
 
-        def weave(eng, g, lo, hi):
-            word = I32 if eng == "v" else U32
-            src = pair(g)[:].bitcast(word).rearrange("p (u n) -> p n u", u=2)
-            move(eng, group(g, lo, hi)[:].bitcast(word), src[:, lo:hi, :])
+        def finish_vector(lo, hi):
+            nc.vector.tensor_scalar(result[:, lo:hi], banks[lo][:, 0 : hi - lo], bias[:], 0.0, ADD, MAX)
 
-        def cast(eng, l, lo=0, hi=T):
-            if l not in win:
-                win[l] = keep.tile([P, T], BF16, name="win%d" % l, align_bytes=64)
-            move(eng, win[l][:, lo:hi], tables[l][:, lo:hi])
+        def store(lo, hi):
+            nc.sync.dma_start(out[:, lo:hi], result[:, lo:hi])
 
-        def code_tiles(g, lo, hi, slot=None):
-            key = (g, lo, hi)
-            codes[key] = keep.tile([P, hi - lo], U32, name=slot or "codes%d_%d_%d" % key, align_bytes=64)
-            scales[key] = keep.tile([P, hi - lo], U8, name="scales%d_%d_%d" % key, align_bytes=64)
-
-        def q(key, lo, hi):
-            first = key[1]
-            if key not in codes:
-                code_tiles(*key)
-            nc.vector.quantize_mx(out=codes[key][:, lo - first : hi - first].bitcast(FP8X4),
-                                  scales=scales[key][:, lo - first : hi - first],
-                                  in_=group(key[0], lo, hi)[:].rearrange("p n j -> p (n j)"))
-
-        def wcopy(eng, g, lo=0, hi=N):
-            if g not in wg:
-                wg[g] = keep.tile([P, N, 4], BF16, name="wg%d" % g, align_bytes=64)
-            if eng == "g":
-                move(eng, wg[g][:, lo:hi], wraw[g][:, :, lo:hi].rearrange("p j m -> p m j"))
-            else:
-                move(eng, wg[g][:, lo:hi].rearrange("p (c i) j -> p c j i", i=4),
-                     wraw[g][:, :, lo:hi].rearrange("p j (c i) -> p c j i", i=4))
-
-        def loadw_halves(g):
-            for h in (0, 1):
-                wraw[g, h] = keep.tile([P, 2, N], F32, name="wraw%d_%d" % (g, h), align_bytes=64)
-                nc.sync.dma_start(wraw[g, h][:], wrows[g][:, 2 * h : 2 * h + 2, :])
-
-        def wcopy_half(eng, g, h):
-            if g not in wg:
-                wg[g] = keep.tile([P, N, 4], BF16, name="wg%d" % g, align_bytes=64)
-            move(eng, wg[g][:, :, 2 * h : 2 * h + 2], wraw[g, h][:].rearrange("p j m -> p m j"))
-
-        def wq(g):
-            nc.vector.quantize_mx(out=wcodes[g][:].bitcast(FP8X4), scales=wscales[g][:],
-                                  in_=wg[g][:].rearrange("p m j -> p (m j)"))
-
-        def mm(key, bank, lo, hi, start, stop):
-            g, first = key[0], key[1]
-            nc.tensor.matmul_mx(out=banks[bank][:, 0 : hi - lo], lhsT=wcodes[g][:].bitcast(FP8X4), lhsT_scale=wscales[g][:],
-                                rhs=codes[key][:, lo - first : hi - first].bitcast(FP8X4),
-                                rhs_scale=scales[key][:, lo - first : hi - first], start=start, stop=stop)
-
-        def fin(eng, bank, lo, hi):
-            if eng == "s":
-                nc.scalar.activation(res[:, lo:hi], banks[bank][:, 0 : hi - lo], RELU, bias=bias[:])
-            else:
-                nc.vector.tensor_scalar(res[:, lo:hi], banks[bank][:, 0 : hi - lo], bias[:], 0.0, ADD, MAX)
-
-        def store(dma, lo, hi):
-            (nc.sync if dma == "y" else nc.scalar).dma_start(out[:, lo:hi], res[:, lo:hi])
-
-        loadw(0, nc.scalar)
-        load(1, nc.scalar)
-        nc.vector.memset(warm[:], 0.0)
-        nc.scalar.activation(warm2[:], warm[:], RELU)
-        pieces = ((0, 128), (128, 256), (256, 384), (384, 512))
-        for l in (0, 2, 3, 4, 5, 6, 7):
-            (load_halves if l == 5 else load)(l)
-        loadw(1)
+        w_raw0 = load_weights(0, nc.scalar)
+        tables = {1: load_table(1, nc.scalar)}
+        for level in (0, 2, 3, 4):
+            tables[level] = load_table(level, nc.sync)
+        table5_halves = [load_table(5, nc.sync, lo, lo + T // 2) for lo in (0, T // 2)]
+        for level in (6, 7):
+            tables[level] = load_table(level, nc.sync)
+        w_raw1 = load_weights(1, nc.sync)
         nc.sync.dma_start(bias[:], b)
-        wcopy("s", 0)
-        wq(0)
-        cast("v", 0)
-        gs(0)
-        cast("v", 1)
-        gs(1)
-        gv(2)
-        gv(3, 0, 256)
-        gv(3, 256, 512)
-        cast("v", 4)
-        weave("s", 0, 0, 256)
-        weave("s", 0, 256, 512)
-        gs(4)
-        cast_half("v", 5, 0)
-        cast_half("v", 5, 1)
-        code_tiles(0, 0, V, slot="table5_0")
-        q((0, 0, V), 0, 256)
-        q((0, 0, V), 256, 512)
-        for c, (lo, hi) in enumerate(pieces):
-            mm((0, 0, V), c, lo, hi, True, False)
-        gs(5)
-        gv(6)
+
+        w_grouped0 = sbuf([P, N, PACK], BF16, "w_grouped0")
+        nc.scalar.copy(w_grouped0[:].rearrange("p (c i) t -> p c t i", i=4),
+                       w_raw0[:].rearrange("p t (c i) -> p c t i", i=4))
+        quantise_weights(0, w_grouped0)
+
+        rounded0 = round_table(0, tables[0])
+        pairs0 = sbuf([P, PACK * V], BF16, "pairs0")
+        look_up_scalar(pairs0, rounded0, 0)
+        look_up_scalar(pairs0, round_table(1, tables[1]), 1)
+        look_up_vector(pairs0, tables[2], 2)
+        halves = [(0, HALF), (HALF, V)]
+        for lo, hi in halves:
+            look_up_vector(pairs0, tables[3], 3, lo, hi)
+
+        rounded4 = round_table(4, tables[4])
+        woven0 = [weave(pairs0, 0, lo, hi) for lo, hi in halves]
+        pairs1 = sbuf([P, PACK * V], BF16, "pairs1")
+        look_up_scalar(pairs1, rounded4, 4)
+        rounded5 = sbuf([P, T], BF16, "rounded5")
+        for half, lo in zip(table5_halves, (0, T // 2)):
+            nc.vector.tensor_copy(rounded5[:, lo : lo + T // 2], half[:])
+        tiles0 = code_tiles(0, 0, V, "table5_0")
+        for woven, (lo, hi) in zip(woven0, halves):
+            quantise_points(tiles0, woven, lo, hi)
         for lo, hi in pieces:
-            gv(7, lo, hi)
+            multiply(0, tiles0, lo, hi)
+
+        look_up_scalar(pairs1, rounded5, 5)
+        look_up_vector(pairs1, tables[6], 6)
         for lo, hi in pieces:
-            weave("s", 1, lo, hi)
-        wcopy("g", 1)
-        q((1, 0, 128), 0, 128)
-        wq(1)
-        mm((1, 0, 128), 0, 0, 128, False, True)
-        code_tiles(1, 128, V, slot="wraw1")
-        for c, (lo, hi) in enumerate(pieces[1:]):
-            q((1, 128, V), lo, hi)
-            mm((1, 128, V), c + 1, lo, hi, False, True)
-        fin("s", 0, 0, 128)
-        fin("s", 1, 128, 256)
-        store("y", 0, 256)
-        fin("s", 2, 256, 384)
-        store("y", 256, 384)
-        fin("v", 3, 384, 512)
-        store("y", 384, 512)
+            look_up_vector(pairs1, tables[7], 7, lo, hi)
+        woven1 = [weave(pairs1, 1, lo, hi) for lo, hi in pieces]
+
+        w_grouped1 = sbuf([P, N, PACK], BF16, "w_grouped1")
+        nc.gpsimd.tensor_scalar(w_grouped1[:], w_raw1[:].rearrange("p t m -> p m t"), 1.0, 0.0, MULT, ADD)
+
+        first_tiles = code_tiles(1, 0, PIECE, "x_codes1_0")
+        quantise_points(first_tiles, woven1[0], 0, PIECE)
+        quantise_weights(1, w_grouped1)
+        multiply(1, first_tiles, 0, PIECE)
+        later_tiles = code_tiles(1, PIECE, V, "w_raw1")
+        for woven, (lo, hi) in zip(woven1[1:], pieces[1:]):
+            quantise_points(later_tiles, woven, lo, hi)
+            multiply(1, later_tiles, lo, hi)
+
+        for lo, hi in pieces[:2]:
+            finish_scalar(lo, hi)
+        store(0, 2 * PIECE)
+        finish_scalar(*pieces[2])
+        store(*pieces[2])
+        finish_vector(*pieces[3])
+        store(*pieces[3])

@@ -62,14 +62,14 @@ def tile_picked_grid_lin_relu_sub_l_kernel(tc, xT, w, b, offs, out):
             return pairs[:, first + 2 * lo : first + 2 * hi - 1 : 2]
 
         def look_up_vector(pairs, table, level, lo=0, hi=V):
-            nc.vector.tensor_copy(pair_places(pairs, level, lo, hi), table[:].indirect(entries(level, lo, hi)))
+            nc.vector.tensor_copy(pair_places(pairs, level, lo, hi), table.indirect(entries(level, lo, hi)))
 
         def look_up_scalar(pairs, rounded, level):
             nc.scalar.activation(pair_places(pairs, level, 0, V), rounded[:].indirect(entries(level, 0, V)), COPY)
 
         def round_table(level, table):
             rounded = sbuf([P, T], BF16, "rounded%d" % level)
-            nc.vector.tensor_copy(rounded[:], table[:])
+            nc.vector.tensor_copy(rounded[:], table)
             return rounded
 
         def weave(pairs, g, lo, hi):
@@ -106,20 +106,19 @@ def tile_picked_grid_lin_relu_sub_l_kernel(tc, xT, w, b, offs, out):
         def store(lo, hi):
             nc.sync.dma_start(out[:, lo:hi], result[:, lo:hi])
 
-        w_raw0 = load_weights(0, nc.scalar)
-        tables = {1: load_table(1, nc.scalar)}
-        for level in (0, 2, 3, 4):
-            tables[level] = load_table(level, nc.sync)
-        table5_halves = [load_table(5, nc.sync, lo, lo + T // 2) for lo in (0, T // 2)]
-        for level in (6, 7):
-            tables[level] = load_table(level, nc.sync)
+        first_two = sbuf([P, 2 * T], F32, "tables01")
+        nc.sync.dma_start(first_two[:], xT.rearrange("(g p u e) c -> g u p (e c)", g=2, u=2, e=2)[0, 0])
+        tables = {0: first_two[:, 0:T], 1: first_two[:, T : 2 * T]}
+        for level in (2, 3):
+            tables[level] = load_table(level, nc.sync)[:]
+        w_raw0 = load_weights(0, nc.sync)
+        for level in range(PACK, LEVELS):
+            tables[level] = load_table(level, nc.sync)[:]
         w_raw1 = load_weights(1, nc.sync)
         nc.sync.dma_start(bias[:], b)
 
         w_grouped0 = sbuf([P, N, PACK], BF16, "w_grouped0")
-        nc.scalar.copy(w_grouped0[:].rearrange("p (c i) t -> p c t i", i=4),
-                       w_raw0[:].rearrange("p t (c i) -> p c t i", i=4))
-        quantise_weights(0, w_grouped0)
+        nc.gpsimd.tensor_scalar(w_grouped0[:], w_raw0[:].rearrange("p t m -> p m t"), 1.0, 0.0, MULT, ADD)
 
         rounded0 = round_table(0, tables[0])
         pairs0 = sbuf([P, PACK * V], BF16, "pairs0")
@@ -134,16 +133,14 @@ def tile_picked_grid_lin_relu_sub_l_kernel(tc, xT, w, b, offs, out):
         woven0 = [weave(pairs0, 0, lo, hi) for lo, hi in halves]
         pairs1 = sbuf([P, PACK * V], BF16, "pairs1")
         look_up_scalar(pairs1, rounded4, 4)
-        rounded5 = sbuf([P, T], BF16, "rounded5")
-        for half, lo in zip(table5_halves, (0, T // 2)):
-            nc.vector.tensor_copy(rounded5[:, lo : lo + T // 2], half[:])
-        tiles0 = code_tiles(0, 0, V, "table5_0")
+        quantise_weights(0, w_grouped0)
+        tiles0 = code_tiles(0, 0, V, "x_codes0")
         for woven, (lo, hi) in zip(woven0, halves):
             quantise_points(tiles0, woven, lo, hi)
         for lo, hi in pieces:
             multiply(0, tiles0, lo, hi)
 
-        look_up_scalar(pairs1, rounded5, 5)
+        look_up_scalar(pairs1, round_table(5, tables[5]), 5)
         look_up_vector(pairs1, tables[6], 6)
         for lo, hi in pieces:
             look_up_vector(pairs1, tables[7], 7, lo, hi)

@@ -106,19 +106,16 @@ def tile_picked_grid_lin_relu_sub_l_kernel(tc, xT, w, b, offs, out):
         def store(lo, hi):
             nc.sync.dma_start(out[:, lo:hi], result[:, lo:hi])
 
-        first_two = sbuf([P, 2 * T], F32, "tables01")
-        nc.sync.dma_start(first_two[:], xT.rearrange("(g p u e) c -> g u p (e c)", g=2, u=2, e=2)[0, 0])
-        tables = {0: first_two[:, 0:T], 1: first_two[:, T : 2 * T]}
-        for level in (2, 3):
+        tables = {1: load_table(1, nc.scalar)[:]}
+        for level in (0, 2, 3, 4):
             tables[level] = load_table(level, nc.sync)[:]
         w_raw0 = load_weights(0, nc.sync)
-        for level in range(PACK, LEVELS):
+        for level in range(5, LEVELS):
             tables[level] = load_table(level, nc.sync)[:]
         w_raw1 = load_weights(1, nc.sync)
         nc.sync.dma_start(bias[:], b)
 
         w_grouped0 = sbuf([P, N, PACK], BF16, "w_grouped0")
-        nc.gpsimd.tensor_scalar(w_grouped0[:], w_raw0[:].rearrange("p t m -> p m t"), 1.0, 0.0, MULT, ADD)
 
         rounded0 = round_table(0, tables[0])
         pairs0 = sbuf([P, PACK * V], BF16, "pairs0")
@@ -133,10 +130,12 @@ def tile_picked_grid_lin_relu_sub_l_kernel(tc, xT, w, b, offs, out):
         woven0 = [weave(pairs0, 0, lo, hi) for lo, hi in halves]
         pairs1 = sbuf([P, PACK * V], BF16, "pairs1")
         look_up_scalar(pairs1, rounded4, 4)
-        quantise_weights(0, w_grouped0)
         tiles0 = code_tiles(0, 0, V, "x_codes0")
-        for woven, (lo, hi) in zip(woven0, halves):
-            quantise_points(tiles0, woven, lo, hi)
+        quantise_points(tiles0, woven0[0], *halves[0])
+        nc.vector.tensor_copy(w_grouped0[:].rearrange("p (c i) t -> p c t i", i=4),
+                              w_raw0[:].rearrange("p t (c i) -> p c t i", i=4))
+        quantise_points(tiles0, woven0[1], *halves[1])
+        quantise_weights(0, w_grouped0)
         for lo, hi in pieces:
             multiply(0, tiles0, lo, hi)
 

@@ -109,9 +109,10 @@ def tile_picked_grid_lin_relu_sub_l_kernel(tc, xT, w, b, offs, out):
         tables = {1: load_table(1, nc.scalar)[:]}
         for level in (0, 2, 3, 4):
             tables[level] = load_table(level, nc.sync)[:]
-        w_raw0 = load_weights(0, nc.sync)
-        for level in range(5, LEVELS):
+        for level in (5, 6):
             tables[level] = load_table(level, nc.sync)[:]
+        w_raw0 = load_weights(0, nc.sync)
+        tables[7] = load_table(7, nc.sync)[:]
         w_raw1 = load_weights(1, nc.sync)
         nc.sync.dma_start(bias[:], b)
 
@@ -132,15 +133,14 @@ def tile_picked_grid_lin_relu_sub_l_kernel(tc, xT, w, b, offs, out):
         look_up_scalar(pairs1, rounded4, 4)
         tiles0 = code_tiles(0, 0, V, "x_codes0")
         quantise_points(tiles0, woven0[0], *halves[0])
-        nc.vector.tensor_copy(w_grouped0[:].rearrange("p (c i) t -> p c t i", i=4),
-                              w_raw0[:].rearrange("p t (c i) -> p c t i", i=4))
         quantise_points(tiles0, woven0[1], *halves[1])
-        quantise_weights(0, w_grouped0)
-        for lo, hi in pieces:
-            multiply(0, tiles0, lo, hi)
 
         look_up_scalar(pairs1, round_table(5, tables[5]), 5)
         look_up_vector(pairs1, tables[6], 6)
+        nc.gpsimd.tensor_scalar(w_grouped0[:], w_raw0[:].rearrange("p t m -> p m t"), 1.0, 0.0, MULT, ADD)
+        quantise_weights(0, w_grouped0)
+        for lo, hi in pieces:
+            multiply(0, tiles0, lo, hi)
         for lo, hi in pieces:
             look_up_vector(pairs1, tables[7], 7, lo, hi)
         woven1 = [weave(pairs1, 1, lo, hi) for lo, hi in pieces]

@@ -106,8 +106,11 @@ def tile_picked_grid_lin_relu_sub_l_kernel(tc, xT, w, b, offs, out):
         def store(lo, hi):
             nc.sync.dma_start(out[:, lo:hi], result[:, lo:hi])
 
-        tables = {1: load_table(1, nc.scalar)[:]}
-        for level in (0, 2, 3, 4):
+        tables = {0: load_table(0, nc.scalar)[:]}
+        both = sbuf([P, 2 * T], F32, "tables12")
+        nc.sync.dma_start(both[:], xT.rearrange("(g p t) c -> g p (t c)", g=2, t=PACK)[0][:, T : 3 * T])
+        tables[1], tables[2] = both[:, :T], both[:, T:]
+        for level in (3, 4):
             tables[level] = load_table(level, nc.sync)[:]
         for level in (5, 6):
             tables[level] = load_table(level, nc.sync)[:]

@@ -33,26 +33,19 @@ def tile_picked_grid_lin_relu_sub_l_kernel(tc, xT, w, b, offs, out):
         offsets = keep.tile([P, LEVELS * V // STRIPE], U16, name="offsets")
         nc.sync.dma_start(offsets[:], offs)
         bias = keep.tile([P, 1], F32, name="bias")
-        x_rows = xT.rearrange("(g p t) c -> g t p c", g=2, t=PACK)
-        w_rows = w.rearrange("(g p t) m -> g p t m", g=2, t=PACK)
-        w_codes = {}
-        w_scales = {}
-        for g in (0, 1):
-            w_codes[g] = sbuf([P, N], U32, "w_codes%d" % g)
-            w_scales[g] = sbuf([P, N], U8, "w_scales%d" % g)
+        x_rows = xT.rearrange("(g p t) c -> g p (t c)", g=2, t=PACK)
         pieces = [(lo, lo + PIECE) for lo in range(0, V, PIECE)]
+        halves = [(0, HALF), (HALF, V)]
         banks = {lo: psum.tile([P, 512], F32, name="bank%d" % lo) for lo, hi in pieces}
         result = keep.tile([P, V], F32, name="result")
+        tables = {}
 
-        def load_table(level, queue, lo=0, hi=T):
-            table = sbuf([P, hi - lo], F32, "table%d_%d" % (level, lo))
-            queue.dma_start(table[:], x_rows[level // PACK, level % PACK][:, lo:hi])
-            return table
-
-        def load_weights(g, queue):
-            raw = sbuf([P, PACK, N], F32, "w_raw%d" % g)
-            queue.dma_start(raw[:], w_rows[g])
-            return raw
+        def load_tables(first, count, queue):
+            tile = sbuf([P, count * T], F32, "tables%d" % first)
+            t = first % PACK
+            queue.dma_start(tile[:], x_rows[first // PACK][:, t * T : (t + count) * T])
+            for i in range(count):
+                tables[first + i] = tile[:, i * T : (i + 1) * T]
 
         def entries(level, lo, hi):
             return offsets[:, (level * V + lo) // STRIPE : (level * V + hi) // STRIPE]
@@ -61,41 +54,34 @@ def tile_picked_grid_lin_relu_sub_l_kernel(tc, xT, w, b, offs, out):
             first = level % PACK // 2 * 2 * V + level % 2
             return pairs[:, first + 2 * lo : first + 2 * hi - 1 : 2]
 
-        def look_up_vector(pairs, table, level, lo=0, hi=V):
-            nc.vector.tensor_copy(pair_places(pairs, level, lo, hi), table.indirect(entries(level, lo, hi)))
+        def look_up_vector(places, level, lo, hi):
+            nc.vector.tensor_copy(places, tables[level].indirect(entries(level, lo, hi)))
 
-        def look_up_scalar(pairs, rounded, level):
-            nc.scalar.activation(pair_places(pairs, level, 0, V), rounded[:].indirect(entries(level, 0, V)), COPY)
+        def look_up_scalar(places, rounded, level, lo, hi):
+            nc.scalar.activation(places, rounded[:].indirect(entries(level, lo, hi)), COPY)
 
-        def round_table(level, table):
-            rounded = sbuf([P, T], BF16, "rounded%d" % level)
-            nc.vector.tensor_copy(rounded[:], table)
+        def round_table(level, tag=None):
+            rounded = sbuf([P, T], BF16, tag or "rounded%d" % level)
+            nc.vector.tensor_copy(rounded[:], tables[level])
             return rounded
 
-        def weave(pairs, g, lo, hi):
+        def weave(pairs, lo, hi, tag, copy=nc.scalar.copy):
             words = pairs[:].bitcast(U32).rearrange("p (u v) -> p v u", u=2)
-            woven = sbuf([P, hi - lo, PACK], BF16, "woven%d_%d" % (g, lo))
-            nc.scalar.copy(woven[:].bitcast(U32), words[:, lo:hi, :])
+            woven = sbuf([P, hi - lo, PACK], BF16, tag)
+            copy(woven[:].bitcast(U32), words[:, lo:hi, :])
             return woven
 
-        def code_tiles(g, lo, hi, tag):
-            return sbuf([P, hi - lo], U32, tag), sbuf([P, hi - lo], U8, "x_scales%d_%d" % (g, lo)), lo
+        def quantise(woven, width, tag):
+            codes = sbuf([P, width], U32, tag)
+            scales = sbuf([P, width], U8, tag + "_scales")
+            nc.vector.quantize_mx(out=codes[:].bitcast(FP8X4), scales=scales[:], in_=woven[:].rearrange("p v t -> p (v t)"))
+            return codes, scales
 
-        def quantise_points(tiles, woven, lo, hi):
-            codes, scales, first = tiles
-            nc.vector.quantize_mx(out=codes[:, lo - first : hi - first].bitcast(FP8X4),
-                                  scales=scales[:, lo - first : hi - first],
-                                  in_=woven[:].rearrange("p v t -> p (v t)"))
-
-        def quantise_weights(g, grouped):
-            nc.vector.quantize_mx(out=w_codes[g][:].bitcast(FP8X4), scales=w_scales[g][:],
-                                  in_=grouped[:].rearrange("p m t -> p (m t)"))
-
-        def multiply(g, tiles, lo, hi):
-            codes, scales, first = tiles
-            nc.tensor.matmul_mx(out=banks[lo][:, 0 : hi - lo], lhsT=w_codes[g][:].bitcast(FP8X4), lhsT_scale=w_scales[g][:],
-                                rhs=codes[:, lo - first : hi - first].bitcast(FP8X4),
-                                rhs_scale=scales[:, lo - first : hi - first], start=g == 0, stop=g == 1)
+        def multiply(bank, weights, w_lo, points, x_lo, start, stop):
+            nc.tensor.matmul_mx(out=banks[bank][:, 0:PIECE], lhsT=weights[0][:, w_lo : w_lo + N].bitcast(FP8X4),
+                                lhsT_scale=weights[1][:, w_lo : w_lo + N],
+                                rhs=points[0][:, x_lo : x_lo + PIECE].bitcast(FP8X4),
+                                rhs_scale=points[1][:, x_lo : x_lo + PIECE], start=start, stop=stop)
 
         def finish_scalar(lo, hi):
             nc.scalar.activation(result[:, lo:hi], banks[lo][:, 0 : hi - lo], RELU, bias=bias[:])
@@ -106,60 +92,61 @@ def tile_picked_grid_lin_relu_sub_l_kernel(tc, xT, w, b, offs, out):
         def store(lo, hi):
             nc.sync.dma_start(out[:, lo:hi], result[:, lo:hi])
 
-        tables = {0: load_table(0, nc.scalar)[:]}
-        both = sbuf([P, 2 * T], F32, "tables12")
-        nc.sync.dma_start(both[:], xT.rearrange("(g p t) c -> g p (t c)", g=2, t=PACK)[0][:, T : 3 * T])
-        tables[1], tables[2] = both[:, :T], both[:, T:]
-        for level in (3, 4):
-            tables[level] = load_table(level, nc.sync)[:]
-        for level in (5, 6):
-            tables[level] = load_table(level, nc.sync)[:]
+        def load_weights(g, queue):
+            raw = sbuf([P, PACK, N], F32, "w_raw%d" % g)
+            queue.dma_start(raw[:], w.rearrange("(g p t) m -> g p t m", g=2, t=PACK)[g])
+            return raw
+
+        def group_weights(raw, tag):
+            grouped = sbuf([P, N, PACK], BF16, tag)
+            nc.gpsimd.tensor_scalar(grouped[:], raw[:].rearrange("p t m -> p m t"), 1.0, 0.0, MULT, ADD)
+            return grouped
+
+        def round_shared(level, split):
+            rounded = sbuf([P, T], BF16, "rounded%d" % level)
+            nc.scalar.copy(rounded[:, :split], tables[level][:, :split])
+            nc.vector.tensor_copy(rounded[:, split:], tables[level][:, split:])
+            return rounded
+
+        load_tables(0, 1, nc.scalar)
+        load_tables(1, 2, nc.sync)
+        load_tables(3, 1, nc.sync)
+        load_tables(4, 2, nc.sync)
+        load_tables(6, 1, nc.sync)
         w_raw0 = load_weights(0, nc.sync)
-        tables[7] = load_table(7, nc.sync)[:]
+        load_tables(7, 1, nc.sync)
         w_raw1 = load_weights(1, nc.sync)
         nc.sync.dma_start(bias[:], b)
 
-        w_grouped0 = sbuf([P, N, PACK], BF16, "w_grouped0")
-
-        rounded0 = round_table(0, tables[0])
         pairs0 = sbuf([P, PACK * V], BF16, "pairs0")
-        look_up_scalar(pairs0, rounded0, 0)
-        look_up_scalar(pairs0, round_table(1, tables[1]), 1)
-        look_up_vector(pairs0, tables[2], 2)
-        halves = [(0, HALF), (HALF, V)]
+        look_up_scalar(pair_places(pairs0, 0, 0, V), round_table(0), 0, 0, V)
+        look_up_scalar(pair_places(pairs0, 1, 0, V), round_table(1), 1, 0, V)
+        look_up_vector(pair_places(pairs0, 2, 0, V), 2, 0, V)
         for lo, hi in halves:
-            look_up_vector(pairs0, tables[3], 3, lo, hi)
-
-        rounded4 = round_table(4, tables[4])
-        woven0 = [weave(pairs0, 0, lo, hi) for lo, hi in halves]
+            look_up_vector(pair_places(pairs0, 3, lo, hi), 3, lo, hi)
+        woven0 = [weave(pairs0, 0, HALF, "woven0_0"), weave(pairs0, HALF, V, "woven0_1", nc.vector.tensor_copy)]
+        points0 = [quantise(woven, HALF, "x0_%d" % i) for i, woven in enumerate(woven0)]
         pairs1 = sbuf([P, PACK * V], BF16, "pairs1")
-        look_up_scalar(pairs1, rounded4, 4)
-        tiles0 = code_tiles(0, 0, V, "x_codes0")
-        quantise_points(tiles0, woven0[0], *halves[0])
-        quantise_points(tiles0, woven0[1], *halves[1])
-
-        look_up_scalar(pairs1, round_table(5, tables[5]), 5)
-        look_up_vector(pairs1, tables[6], 6)
-        nc.gpsimd.tensor_scalar(w_grouped0[:], w_raw0[:].rearrange("p t m -> p m t"), 1.0, 0.0, MULT, ADD)
-        quantise_weights(0, w_grouped0)
+        look_up_scalar(pair_places(pairs1, 4, 0, V), round_shared(4, 640), 4, 0, V)
+        look_up_scalar(pair_places(pairs1, 5, 0, V), round_table(5), 5, 0, V)
+        look_up_vector(pair_places(pairs1, 6, 0, V), 6, 0, V)
+        weights0 = quantise(group_weights(w_raw0, "w_grouped0"), N, "w_codes0")
         for lo, hi in pieces:
-            multiply(0, tiles0, lo, hi)
+            multiply(lo, weights0, 0, points0[lo // HALF], lo % HALF, True, False)
         for lo, hi in pieces:
-            look_up_vector(pairs1, tables[7], 7, lo, hi)
-        woven1 = [weave(pairs1, 1, lo, hi) for lo, hi in pieces]
-
-        w_grouped1 = sbuf([P, N, PACK], BF16, "w_grouped1")
-        nc.gpsimd.tensor_scalar(w_grouped1[:], w_raw1[:].rearrange("p t m -> p m t"), 1.0, 0.0, MULT, ADD)
-
-        first_tiles = code_tiles(1, 0, PIECE, "x_codes1_0")
-        quantise_points(first_tiles, woven1[0], 0, PIECE)
-        quantise_weights(1, w_grouped1)
-        multiply(1, first_tiles, 0, PIECE)
-        later_tiles = code_tiles(1, PIECE, V, "w_raw1")
+            look_up_vector(pair_places(pairs1, 7, lo, hi), 7, lo, hi)
+        woven1 = [weave(pairs1, lo, hi, "woven1_%d" % lo) for lo, hi in pieces]
+        w_grouped1 = group_weights(w_raw1, "w_grouped1")
+        first = quantise(woven1[0], PIECE, "x1_0")
+        weights1 = quantise(w_grouped1, N, "w_codes1")
+        multiply(0, weights1, 0, first, 0, False, True)
+        later_codes = sbuf([P, V - PIECE], U32, "w_raw1")
+        later_scales = sbuf([P, V - PIECE], U8, "x1_later_scales")
         for woven, (lo, hi) in zip(woven1[1:], pieces[1:]):
-            quantise_points(later_tiles, woven, lo, hi)
-            multiply(1, later_tiles, lo, hi)
-
+            nc.vector.quantize_mx(out=later_codes[:, lo - PIECE : hi - PIECE].bitcast(FP8X4),
+                                  scales=later_scales[:, lo - PIECE : hi - PIECE],
+                                  in_=woven[:].rearrange("p v t -> p (v t)"))
+            multiply(lo, weights1, 0, (later_codes, later_scales), lo - PIECE, False, True)
         for lo, hi in pieces[:2]:
             finish_scalar(lo, hi)
         store(0, 2 * PIECE)

@@ -65,16 +65,18 @@ def tile_picked_grid_lin_relu_sub_l_kernel(tc, xT, w, b, offs, out):
             nc.vector.tensor_copy(rounded[:], tables[level])
             return rounded
 
-        def weave(pairs, lo, hi, tag, copy=nc.scalar.copy):
+        def weave(pairs, lo, hi, woven, copy=nc.scalar.copy):
             words = pairs[:].bitcast(U32).rearrange("p (u v) -> p v u", u=2)
-            woven = sbuf([P, hi - lo, PACK], BF16, tag)
-            copy(woven[:].bitcast(U32), words[:, lo:hi, :])
+            copy(woven.bitcast(U32).rearrange("p (v u) -> p v u", u=2), words[:, lo:hi, :])
             return woven
+
+        def woven_tile(width, tag):
+            return sbuf([P, PACK * width], BF16, tag)[:]
 
         def quantise(woven, width, tag):
             codes = sbuf([P, width], U32, tag)
             scales = sbuf([P, width], U8, tag + "_scales")
-            nc.vector.quantize_mx(out=codes[:].bitcast(FP8X4), scales=scales[:], in_=woven[:].rearrange("p v t -> p (v t)"))
+            nc.vector.quantize_mx(out=codes[:].bitcast(FP8X4), scales=scales[:], in_=woven)
             return codes, scales
 
         def multiply(bank, weights, w_lo, points, x_lo, start, stop):
@@ -100,42 +102,47 @@ def tile_picked_grid_lin_relu_sub_l_kernel(tc, xT, w, b, offs, out):
         def group_weights(raw, tag):
             grouped = sbuf([P, N, PACK], BF16, tag)
             nc.gpsimd.tensor_scalar(grouped[:], raw[:].rearrange("p t m -> p m t"), 1.0, 0.0, MULT, ADD)
-            return grouped
+            return grouped[:].rearrange("p m t -> p (m t)")
 
         def round_shared(level, split):
             rounded = sbuf([P, T], BF16, "rounded%d" % level)
             nc.scalar.copy(rounded[:, :split], tables[level][:, :split])
-            nc.vector.tensor_copy(rounded[:, split:], tables[level][:, split:])
+            if split < T:
+                nc.vector.tensor_copy(rounded[:, split:], tables[level][:, split:])
             return rounded
 
         load_tables(0, 1, nc.scalar)
         load_tables(1, 2, nc.sync)
-        load_tables(3, 1, nc.sync)
-        load_tables(4, 2, nc.sync)
-        load_tables(6, 1, nc.sync)
+        apart = K // 2 - 3
+        tables34 = sbuf([P, 2 * T], F32, "tables34")
+        nc.sync.dma_start(tables34[:].rearrange("p (j c) -> p j c", j=2),
+                          xT[3 : 3 + 2 * apart].rearrange("(j q) c -> q j c", j=2)[0:apart:PACK])
+        tables[3], tables[4] = tables34[:, :T], tables34[:, T:]
+        load_tables(5, 2, nc.sync)
         w_raw0 = load_weights(0, nc.sync)
         load_tables(7, 1, nc.sync)
         w_raw1 = load_weights(1, nc.sync)
         nc.sync.dma_start(bias[:], b)
 
         pairs0 = sbuf([P, PACK * V], BF16, "pairs0")
+        pairs1 = sbuf([P, PACK * V], BF16, "pairs1")
         look_up_scalar(pair_places(pairs0, 0, 0, V), round_table(0), 0, 0, V)
         look_up_scalar(pair_places(pairs0, 1, 0, V), round_table(1), 1, 0, V)
         look_up_vector(pair_places(pairs0, 2, 0, V), 2, 0, V)
         for lo, hi in halves:
             look_up_vector(pair_places(pairs0, 3, lo, hi), 3, lo, hi)
-        woven0 = [weave(pairs0, 0, HALF, "woven0_0"), weave(pairs0, HALF, V, "woven0_1", nc.vector.tensor_copy)]
+        look_up_scalar(pair_places(pairs1, 4, 0, V), round_shared(4, T), 4, 0, V)
+        woven0 = [weave(pairs0, 0, HALF, pairs1[:, 2 * V :], nc.vector.tensor_copy),
+                  weave(pairs0, HALF, V, woven_tile(HALF, "woven0_1"), nc.vector.tensor_copy)]
         points0 = [quantise(woven, HALF, "x0_%d" % i) for i, woven in enumerate(woven0)]
-        pairs1 = sbuf([P, PACK * V], BF16, "pairs1")
-        look_up_scalar(pair_places(pairs1, 4, 0, V), round_shared(4, 640), 4, 0, V)
-        look_up_scalar(pair_places(pairs1, 5, 0, V), round_table(5), 5, 0, V)
+        look_up_scalar(pair_places(pairs1, 5, 0, V), round_shared(5, 384), 5, 0, V)
         look_up_vector(pair_places(pairs1, 6, 0, V), 6, 0, V)
         weights0 = quantise(group_weights(w_raw0, "w_grouped0"), N, "w_codes0")
         for lo, hi in pieces:
             multiply(lo, weights0, 0, points0[lo // HALF], lo % HALF, True, False)
         for lo, hi in pieces:
             look_up_vector(pair_places(pairs1, 7, lo, hi), 7, lo, hi)
-        woven1 = [weave(pairs1, lo, hi, "woven1_%d" % lo) for lo, hi in pieces]
+        woven1 = [weave(pairs1, lo, hi, woven_tile(PIECE, "woven1_%d" % lo)) for lo, hi in pieces]
         w_grouped1 = group_weights(w_raw1, "w_grouped1")
         first = quantise(woven1[0], PIECE, "x1_0")
         weights1 = quantise(w_grouped1, N, "w_codes1")
@@ -145,7 +152,7 @@ def tile_picked_grid_lin_relu_sub_l_kernel(tc, xT, w, b, offs, out):
         for woven, (lo, hi) in zip(woven1[1:], pieces[1:]):
             nc.vector.quantize_mx(out=later_codes[:, lo - PIECE : hi - PIECE].bitcast(FP8X4),
                                   scales=later_scales[:, lo - PIECE : hi - PIECE],
-                                  in_=woven[:].rearrange("p v t -> p (v t)"))
+                                  in_=woven)
             multiply(lo, weights1, 0, (later_codes, later_scales), lo - PIECE, False, True)
         for lo, hi in pieces[:2]:
             finish_scalar(lo, hi)

@@ -113,11 +113,8 @@ def tile_picked_grid_lin_relu_sub_l_kernel(tc, xT, w, b, offs, out):
 
         load_tables(0, 1, nc.scalar)
         load_tables(1, 2, nc.sync)
-        apart = K // 2 - 3
-        tables34 = sbuf([P, 2 * T], F32, "tables34")
-        nc.sync.dma_start(tables34[:].rearrange("p (j c) -> p j c", j=2),
-                          xT[3 : 3 + 2 * apart].rearrange("(j q) c -> q j c", j=2)[0:apart:PACK])
-        tables[3], tables[4] = tables34[:, :T], tables34[:, T:]
+        load_tables(3, 1, nc.sync)
+        load_tables(4, 1, nc.sync)
         load_tables(5, 2, nc.sync)
         w_raw0 = load_weights(0, nc.sync)
         load_tables(7, 1, nc.sync)
@@ -131,7 +128,10 @@ def tile_picked_grid_lin_relu_sub_l_kernel(tc, xT, w, b, offs, out):
         look_up_vector(pair_places(pairs0, 2, 0, V), 2, 0, V)
         for lo, hi in halves:
             look_up_vector(pair_places(pairs0, 3, lo, hi), 3, lo, hi)
-        look_up_scalar(pair_places(pairs1, 4, 0, V), round_shared(4, T), 4, 0, V)
+        rounded4 = sbuf([P, T], BF16, "rounded4")
+        nc.scalar.copy(rounded4[:, : T // 2], tables[4][:, : T // 2])
+        nc.gpsimd.tensor_scalar(rounded4[:, T // 2 :], tables[4][:, T // 2 :], 1.0, 0.0, MULT, ADD)
+        look_up_scalar(pair_places(pairs1, 4, 0, V), rounded4, 4, 0, V)
         woven0 = [weave(pairs0, 0, HALF, pairs1[:, 2 * V :], nc.vector.tensor_copy),
                   weave(pairs0, HALF, V, woven_tile(HALF, "woven0_1"), nc.vector.tensor_copy)]
         points0 = [quantise(woven, HALF, "x0_%d" % i) for i, woven in enumerate(woven0)]

@@ -154,10 +154,10 @@ def tile_picked_grid_lin_relu_sub_l_kernel(tc, xT, w, b, offs, out):
                                   scales=later_scales[:, lo - PIECE : hi - PIECE],
                                   in_=woven)
             multiply(lo, weights1, 0, (later_codes, later_scales), lo - PIECE, False, True)
-        for lo, hi in pieces[:2]:
+        finish_scalar(*pieces[0])
+        store(*pieces[0])
+        for lo, hi in pieces[1:3]:
             finish_scalar(lo, hi)
-        store(0, 2 * PIECE)
-        finish_scalar(*pieces[2])
-        store(*pieces[2])
+        store(PIECE, 3 * PIECE)
         finish_vector(*pieces[3])
         store(*pieces[3])

@@ -101,7 +101,8 @@ def tile_picked_grid_lin_relu_sub_l_kernel(tc, xT, w, b, offs, out):
 
         def group_weights(raw, tag):
             grouped = sbuf([P, N, PACK], BF16, tag)
-            nc.gpsimd.tensor_scalar(grouped[:], raw[:].rearrange("p t m -> p m t"), 1.0, 0.0, MULT, ADD)
+            nc.gpsimd.tensor_scalar(grouped[:].rearrange("p (c i) t -> p c t i", i=2),
+                                    raw[:].rearrange("p t (c i) -> p c t i", i=2), 1.0, 0.0, MULT, ADD)
             return grouped[:].rearrange("p m t -> p (m t)")
 
         def round_shared(level, split):

@@ -155,10 +155,9 @@ def tile_picked_grid_lin_relu_sub_l_kernel(tc, xT, w, b, offs, out):
                                   scales=later_scales[:, lo - PIECE : hi - PIECE],
                                   in_=woven)
             multiply(lo, weights1, 0, (later_codes, later_scales), lo - PIECE, False, True)
-        finish_scalar(*pieces[0])
-        store(*pieces[0])
-        for lo, hi in pieces[1:3]:
+        for lo, hi in pieces[:2]:
             finish_scalar(lo, hi)
-        store(PIECE, 3 * PIECE)
-        finish_vector(*pieces[3])
-        store(*pieces[3])
+            store(lo, hi)
+        for lo, hi in pieces[2:]:
+            finish_vector(lo, hi)
+        store(HALF, V)

from contextlib import ExitStack

import concourse.mybir as mybir

K, T, V, N = 1024, 1024, 512, 128
LEVELS = 8
FLOPS = 2 * K * N * V
P = 128
PACK = 4
STRIPE = 16
HALF = V // 2
PIECE = 128
F32 = mybir.dt.float32
BF16 = mybir.dt.bfloat16
U32 = mybir.dt.uint32
U16 = mybir.dt.uint16
U8 = mybir.dt.uint8
FP8X4 = mybir.dt.float8_e4m3fn_x4
COPY = mybir.ActivationFunctionType.Copy
RELU = mybir.ActivationFunctionType.Relu
MULT, ADD, MAX = mybir.AluOpType.mult, mybir.AluOpType.add, mybir.AluOpType.max


def tile_picked_grid_lin_relu_sub_l_kernel(tc, xT, w, b, offs, out):
    nc = tc.nc
    with ExitStack() as ctx:
        keep = ctx.enter_context(tc.tile_pool(name="keep", bufs=1))
        psum = ctx.enter_context(tc.psum_pool(name="psum", bufs=1))

        def sbuf(shape, dtype, tag):
            return keep.tile(shape, dtype, name=tag, align_bytes=64)

        offsets = keep.tile([P, LEVELS * V // STRIPE], U16, name="offsets")
        nc.sync.dma_start(offsets[:], offs)
        bias = keep.tile([P, 1], F32, name="bias")
        x_rows = xT.rearrange("(g p t) c -> g p (t c)", g=2, t=PACK)
        pieces = [(lo, lo + PIECE) for lo in range(0, V, PIECE)]
        halves = [(0, HALF), (HALF, V)]
        banks = {lo: psum.tile([P, 512], F32, name="bank%d" % lo) for lo, hi in pieces}
        result = keep.tile([P, V], F32, name="result")
        tables = {}

        def load_tables(first, count, queue):
            tile = sbuf([P, count * T], F32, "tables%d" % first)
            t = first % PACK
            queue.dma_start(tile[:], x_rows[first // PACK][:, t * T : (t + count) * T])
            for i in range(count):
                tables[first + i] = tile[:, i * T : (i + 1) * T]

        def entries(level, lo, hi):
            return offsets[:, (level * V + lo) // STRIPE : (level * V + hi) // STRIPE]

        def pair_places(pairs, level, lo, hi):
            first = level % PACK // 2 * 2 * V + level % 2
            return pairs[:, first + 2 * lo : first + 2 * hi - 1 : 2]

        def look_up_vector(places, level, lo, hi):
            nc.vector.tensor_copy(places, tables[level].indirect(entries(level, lo, hi)))

        def look_up_scalar(places, rounded, level, lo, hi):
            nc.scalar.activation(places, rounded[:].indirect(entries(level, lo, hi)), COPY)

        def round_table(level, tag=None):
            rounded = sbuf([P, T], BF16, tag or "rounded%d" % level)
            nc.vector.tensor_copy(rounded[:], tables[level])
            return rounded

        def weave(pairs, lo, hi, woven, copy=nc.scalar.copy):
            words = pairs[:].bitcast(U32).rearrange("p (u v) -> p v u", u=2)
            copy(woven.bitcast(U32).rearrange("p (v u) -> p v u", u=2), words[:, lo:hi, :])
            return woven

        def woven_tile(width, tag):
            return sbuf([P, PACK * width], BF16, tag)[:]

        def quantise(woven, width, tag):
            codes = sbuf([P, width], U32, tag)
            scales = sbuf([P, width], U8, tag + "_scales")
            nc.vector.quantize_mx(out=codes[:].bitcast(FP8X4), scales=scales[:], in_=woven)
            return codes, scales

        def multiply(bank, weights, w_lo, points, x_lo, start, stop):
            nc.tensor.matmul_mx(out=banks[bank][:, 0:PIECE], lhsT=weights[0][:, w_lo : w_lo + N].bitcast(FP8X4),
                                lhsT_scale=weights[1][:, w_lo : w_lo + N],
                                rhs=points[0][:, x_lo : x_lo + PIECE].bitcast(FP8X4),
                                rhs_scale=points[1][:, x_lo : x_lo + PIECE], start=start, stop=stop)

        def finish_scalar(lo, hi):
            nc.scalar.activation(result[:, lo:hi], banks[lo][:, 0 : hi - lo], RELU, bias=bias[:])

        def finish_vector(lo, hi):
            nc.vector.tensor_scalar(result[:, lo:hi], banks[lo][:, 0 : hi - lo], bias[:], 0.0, ADD, MAX)

        def store(lo, hi):
            nc.sync.dma_start(out[:, lo:hi], result[:, lo:hi])

        def load_weights(g, queue):
            raw = sbuf([P, PACK, N], F32, "w_raw%d" % g)
            queue.dma_start(raw[:], w.rearrange("(g p t) m -> g p t m", g=2, t=PACK)[g])
            return raw

        def group_weights(raw, tag):
            grouped = sbuf([P, N, PACK], BF16, tag)
            nc.gpsimd.tensor_scalar(grouped[:].rearrange("p (c i) t -> p c t i", i=2),
                                    raw[:].rearrange("p t (c i) -> p c t i", i=2), 1.0, 0.0, MULT, ADD)
            return grouped[:].rearrange("p m t -> p (m t)")

        def round_shared(level, split):
            rounded = sbuf([P, T], BF16, "rounded%d" % level)
            nc.scalar.copy(rounded[:, :split], tables[level][:, :split])
            if split < T:
                nc.vector.tensor_copy(rounded[:, split:], tables[level][:, split:])
            return rounded

        load_tables(0, 1, nc.scalar)
        load_tables(1, 2, nc.sync)
        load_tables(3, 1, nc.sync)
        load_tables(4, 1, nc.sync)
        load_tables(5, 2, nc.sync)
        w_raw0 = load_weights(0, nc.sync)
        load_tables(7, 1, nc.sync)
        w_raw1 = load_weights(1, nc.sync)
        nc.sync.dma_start(bias[:], b)

        pairs0 = sbuf([P, PACK * V], BF16, "pairs0")
        pairs1 = sbuf([P, PACK * V], BF16, "pairs1")
        look_up_scalar(pair_places(pairs0, 0, 0, V), round_table(0), 0, 0, V)
        look_up_scalar(pair_places(pairs0, 1, 0, V), round_table(1), 1, 0, V)
        look_up_vector(pair_places(pairs0, 2, 0, V), 2, 0, V)
        for lo, hi in halves:
            look_up_vector(pair_places(pairs0, 3, lo, hi), 3, lo, hi)
        rounded4 = sbuf([P, T], BF16, "rounded4")
        nc.scalar.copy(rounded4[:, : T // 2], tables[4][:, : T // 2])
        nc.gpsimd.tensor_scalar(rounded4[:, T // 2 :], tables[4][:, T // 2 :], 1.0, 0.0, MULT, ADD)
        look_up_scalar(pair_places(pairs1, 4, 0, V), rounded4, 4, 0, V)
        woven0 = [weave(pairs0, 0, HALF, pairs1[:, 2 * V :], nc.vector.tensor_copy),
                  weave(pairs0, HALF, V, woven_tile(HALF, "woven0_1"), nc.vector.tensor_copy)]
        points0 = [quantise(woven, HALF, "x0_%d" % i) for i, woven in enumerate(woven0)]
        look_up_scalar(pair_places(pairs1, 5, 0, V), round_shared(5, 384), 5, 0, V)
        look_up_vector(pair_places(pairs1, 6, 0, V), 6, 0, V)
        weights0 = quantise(group_weights(w_raw0, "w_grouped0"), N, "w_codes0")
        for lo, hi in pieces:
            multiply(lo, weights0, 0, points0[lo // HALF], lo % HALF, True, False)
        for lo, hi in pieces:
            look_up_vector(pair_places(pairs1, 7, lo, hi), 7, lo, hi)
        woven1 = [weave(pairs1, lo, hi, woven_tile(PIECE, "woven1_%d" % lo)) for lo, hi in pieces]
        w_grouped1 = group_weights(w_raw1, "w_grouped1")
        first = quantise(woven1[0], PIECE, "x1_0")
        weights1 = quantise(w_grouped1, N, "w_codes1")
        multiply(0, weights1, 0, first, 0, False, True)
        later_codes = sbuf([P, V - PIECE], U32, "w_raw1")
        later_scales = sbuf([P, V - PIECE], U8, "x1_later_scales")
        for woven, (lo, hi) in zip(woven1[1:], pieces[1:]):
            nc.vector.quantize_mx(out=later_codes[:, lo - PIECE : hi - PIECE].bitcast(FP8X4),
                                  scales=later_scales[:, lo - PIECE : hi - PIECE],
                                  in_=woven)
            multiply(lo, weights1, 0, (later_codes, later_scales), lo - PIECE, False, True)
        for lo, hi in pieces[:2]:
            finish_scalar(lo, hi)
            store(lo, hi)
        for lo, hi in pieces[2:]:
            finish_vector(lo, hi)
        store(HALF, V)
